import numpy as np
import ml_dtypes


def mxq(x, axis, fmt="e4m3"):
    dtype, down = {"e4m3": (ml_dtypes.float8_e4m3fn, 7), "e5m2": (ml_dtypes.float8_e5m2, 14)}[fmt]
    v = np.moveaxis(np.asarray(x, np.float32).astype(ml_dtypes.bfloat16).astype(np.float64), axis, -1)
    blocks = v.reshape(v.shape[:-1] + (-1, 32))
    amax = np.abs(blocks).max(-1, keepdims=True)
    byte = np.maximum(np.where(amax > 0, np.frexp(amax)[1] - 1 + 127, 0) - down, 1)
    scale = np.exp2(byte - 127.0)
    codes = (blocks / scale).astype(np.float32).astype(dtype).astype(np.float64)
    return np.moveaxis((codes * scale).reshape(v.shape), -1, axis)


WIDE = False


def mx_kscale(k):
    if not WIDE:
        return np.ones(k)
    levels = np.array([10, -10, 5, -5, 0])
    if k % 512:
        return np.exp2(np.random.permutation(np.resize(levels, k // 32))).repeat(32)
    a = np.empty((k // 512, 16))
    for p in range(k // 512):
        a[p, :8] = np.random.permutation(np.resize(levels, 8))
        for g in range(8):
            far = levels[np.abs(levels - a[p, g]) >= 10]
            a[p, g + 8] = far[np.random.randint(len(far))]
    return np.exp2(a.ravel()).repeat(32)


def f64(x):
    return np.asarray(x).astype(np.float64)


def striped(idx):
    return np.tile(idx.reshape(-1, 16).T, (8, 1)).astype(np.uint16)


def unstriped(offs):
    return offs[:16].T.reshape(-1).astype(np.int64)


def relu2(v):
    return np.maximum(v, 0.0) ** 2


K, T, E, C, H, N = 1024, 1536, 4, 256, 512, 256


def by_expert(wq, xq):
    return np.concatenate([wq[e].T @ xq[:, e * C:(e + 1) * C] for e in range(E)], axis=1)


def setup_inputs():
    n = np.random.standard_normal
    s = mx_kscale(K)[:, None]
    u = mx_kscale(H)
    return {
        "xT": (n((K, T)) * s).astype(np.float32),
        "w1": (n((E, K, H)) / np.sqrt(K) / s[None] * u[None, None, :]).astype(np.float32),
        "w2": (n((E, H, N)) / np.sqrt(H) / u[None, :, None] ** 2).astype(np.float32),
        "gate": np.tile(np.random.uniform(0.2, 1.0, E * C), (N, 1)).astype(np.float32),
        "offs": striped(np.random.permutation(T)[:E * C]),
    }


def reference(xT, w1, w2, gate, offs):
    idx = unstriped(offs)
    xq = mxq(f64(xT)[:, idx], 0, "e4m3")
    h = relu2(by_expert(mxq(f64(w1), 1, "e4m3"), xq))
    y = by_expert(mxq(f64(w2), 1, "e4m3"), mxq(h, 0, "e4m3"))
    out = np.zeros((N, T))
    out[:, idx] = f64(gate) * y
    return out

@@ -1,0 +1,234 @@
+from contextlib import ExitStack
+
+import concourse.mybir as mybir
+
+K, T, E, C, H, N = 1024, 1536, 4, 256, 512, 256
+FLOPS = 2 * E * C * (K * H + H * N)
+
+F32 = mybir.dt.float32
+BF16 = mybir.dt.bfloat16
+U32 = mybir.dt.uint32
+U16 = mybir.dt.uint16
+U8 = mybir.dt.uint8
+FP8X4 = mybir.dt.float8_e4m3fn_x4
+MULT = mybir.AluOpType.mult
+RELU = mybir.ActivationFunctionType.Relu
+SQUARE = mybir.ActivationFunctionType.Square
+
+P = 128
+PACK = 4
+PASSES = K // (P * PACK)
+TILES = H // P
+BANK_TILES = 2
+OUT_TILES = N // P
+LIST_ROWS = 16
+CHUNK = 512
+
+X_VECTOR = 192
+W1_VECTOR = (0, 64, 32, 48)
+
+
+def interleave(copy, grouped, raw):
+    copy(
+        grouped.rearrange("p (c i) j -> p c j i", i=4),
+        raw.rearrange("p j (c i) -> p c j i", i=4),
+    )
+
+
+def interleave_w1(copy, grouped, raw, first, last):
+    copy(
+        grouped.rearrange("p (t m) j -> p m j t", t=TILES)[:, first:last],
+        raw.rearrange("p j (m t) -> p m j t", t=TILES)[:, first:last],
+    )
+
+
+def tile_routed_moe_kernel(tc, xT, w1, w2, gate, offs, out):
+    nc = tc.nc
+    with ExitStack() as ctx:
+        keep = ctx.enter_context(tc.tile_pool(name="keep", bufs=1))
+        raw_pool = ctx.enter_context(tc.tile_pool(name="raw_pool", bufs=11))
+        x_pool = ctx.enter_context(tc.tile_pool(name="x_pool", bufs=2))
+        w1_pool = ctx.enter_context(tc.tile_pool(name="w1_pool", bufs=2))
+        w2_pool = ctx.enter_context(tc.tile_pool(name="w2_pool", bufs=2))
+        relu_pool = ctx.enter_context(tc.tile_pool(name="relu_pool", bufs=2))
+        h_pool = ctx.enter_context(tc.tile_pool(name="h_pool", bufs=2))
+        h_codes_pool = ctx.enter_context(tc.tile_pool(name="h_codes_pool", bufs=3))
+        y_pool = ctx.enter_context(tc.tile_pool(name="y_pool", bufs=2))
+        h_psum = ctx.enter_context(tc.psum_pool(name="h_psum", bufs=5))
+        y_psum = ctx.enter_context(tc.psum_pool(name="y_psum", bufs=3))
+
+        slots_list = keep.tile([P, E * C // LIST_ROWS], U16, name="slots_list", align_bytes=64)
+        words = [keep.tile([P, T], U32, name=f"words{a}", align_bytes=64) for a in range(PASSES)]
+        scales = keep.tile([P, T], U8, name="scales", align_bytes=64)
+        nc.gpsimd.memset(scales[:], 0)
+        windows = [keep.tile([P, T], F32, name=f"window{b}", align_bytes=64) for b in range(OUT_TILES)]
+        slot_words = keep.tile([P, PASSES, E * C], U32, name="slot_words", align_bytes=64)
+        slot_scales = keep.tile([P, E * C], U8, name="slot_scales", align_bytes=64)
+        gate_sb = keep.tile([P, OUT_TILES, E * C], F32, name="gate_sb", align_bytes=64)
+        w2_words = keep.tile([P, E, N], U32, name="w2_words", align_bytes=64)
+        w2_scales = keep.tile([P, E, N], U8, name="w2_scales", align_bytes=64)
+
+        x_raw, w1_raw, w2_raw, w1_words, w1_scales = {}, {}, {}, {}, {}
+
+        def load_x(a):
+            rows = xT.rearrange("(a p j) n -> a p j n", p=P, j=PACK)[a]
+            for c in range(T // CHUNK):
+                x_raw[a, c] = raw_pool.tile([P, PACK, CHUNK], F32, name="raw", align_bytes=64)
+                nc.sync.dma_start(x_raw[a, c][:], rows[:, :, c * CHUNK : (c + 1) * CHUNK])
+
+        def load_w1(e):
+            for a in range(PASSES):
+                w1_raw[e, a] = raw_pool.tile([P, PACK, H], F32, name="raw", align_bytes=64)
+                nc.sync.dma_start(w1_raw[e, a][:], w1[e].rearrange("(a p j) h -> a p j h", p=P, j=PACK)[a])
+
+        def load_w2(pair):
+            w2_raw[pair] = keep.tile([P, 2, PACK, N], F32, name=f"w2_raw{pair}", align_bytes=64)
+            for i in range(2):
+                nc.sync.dma_start(w2_raw[pair][:, i], w2[2 * pair + i].rearrange("(p j) n -> p j n", j=PACK))
+
+        nc.sync.dma_start(slots_list[:], offs)
+        load_x(0)
+        load_x(1)
+        load_w1(0)
+        load_w2(0)
+        load_w1(1)
+        load_w1(2)
+        nc.sync.dma_start(gate_sb[:], gate.rearrange("(b p) j -> p b j", p=P))
+        load_w1(3)
+        load_w2(1)
+
+        for b in range(OUT_TILES):
+            nc.vector.memset(windows[b][:], 0.0)
+
+        def quantise_x(a):
+            for c in range(T // CHUNK):
+                grouped = x_pool.tile([P, CHUNK, PACK], BF16, name="x_grouped", align_bytes=64)
+                raw = x_raw[a, c]
+                interleave(nc.vector.tensor_copy, grouped[:, :X_VECTOR], raw[:, :, :X_VECTOR])
+                interleave(nc.scalar.copy, grouped[:, X_VECTOR:], raw[:, :, X_VECTOR:])
+                tokens = slice(c * CHUNK, (c + 1) * CHUNK)
+                nc.vector.quantize_mx(
+                    out=words[a][:, tokens].bitcast(FP8X4),
+                    scales=scales[4 * a : P, tokens],
+                    in_=grouped[:].rearrange("p c j -> p (c j)"),
+                )
+
+        def gather_words(a):
+            nc.vector.tensor_copy(slot_words[:, a, :], words[a][:].indirect(slots_list[:]))
+
+        def gather_scales():
+            nc.vector.tensor_copy(slot_scales[:], scales[:].indirect(slots_list[:]))
+
+        def quantise_w1(e):
+            w1_words[e] = keep.tile([P, PASSES, H], U32, name=f"w1_words{e}", align_bytes=64)
+            w1_scales[e] = keep.tile([P, PASSES, H], U8, name=f"w1_scales{e}", align_bytes=64)
+            at_once = PASSES if e == 0 else 1
+            vector = W1_VECTOR[e]
+            for a0 in range(0, PASSES, at_once):
+                grouped = w1_pool.tile([P, at_once, H, PACK], BF16, name="w1_grouped", align_bytes=64)
+                for i in range(at_once):
+                    raw = w1_raw[e, a0 + i][:]
+                    if vector > 0:
+                        interleave_w1(nc.vector.tensor_copy, grouped[:, i], raw, 0, vector)
+                    interleave_w1(nc.scalar.copy, grouped[:, i], raw, vector, P)
+                nc.vector.quantize_mx(
+                    out=w1_words[e][:, a0 : a0 + at_once].rearrange("p a h -> p (a h)").bitcast(FP8X4),
+                    scales=w1_scales[e][:, a0 : a0 + at_once].rearrange("p a h -> p (a h)"),
+                    in_=grouped[:].rearrange("p a h j -> p (a h j)"),
+                )
+
+        def quantise_w2(pair):
+            grouped = w2_pool.tile([P, 2, N, PACK], BF16, name="w2_grouped", align_bytes=64)
+            for i in range(2):
+                interleave(nc.scalar.copy, grouped[:, i], w2_raw[pair][:, i])
+            experts = slice(2 * pair, 2 * pair + 2)
+            nc.vector.quantize_mx(
+                out=w2_words[:, experts].rearrange("p e n -> p (e n)").bitcast(FP8X4),
+                scales=w2_scales[:, experts].rearrange("p e n -> p (e n)"),
+                in_=grouped[:].rearrange("p e n j -> p (e n j)"),
+            )
+
+        def layer1(e):
+            slots = slice(C * e, C * (e + 1))
+            relu = relu_pool.tile([P, TILES // BANK_TILES, C, BANK_TILES], F32, name="relu", align_bytes=64)
+            for u in range(TILES // BANK_TILES):
+                sums = h_psum.tile([P, BANK_TILES, C], F32, name="h_sums")
+                for i in range(BANK_TILES):
+                    t = BANK_TILES * u + i
+                    columns = slice(P * t, P * (t + 1))
+                    for a in range(PASSES):
+                        nc.tensor.matmul_mx(
+                            out=sums[:, i],
+                            lhsT=w1_words[e][:, a, columns].bitcast(FP8X4),
+                            lhsT_scale=w1_scales[e][:, a, columns],
+                            rhs=slot_words[:, a, slots].bitcast(FP8X4),
+                            rhs_scale=slot_scales[4 * a : P, slots],
+                            start=(a == 0),
+                            stop=(a == PASSES - 1),
+                        )
+                nc.scalar.activation(relu[:, u], sums[:].rearrange("p i n -> p n i"), RELU)
+
+            grouped = h_pool.tile([P, C, PACK], BF16, name="h_grouped", align_bytes=64)
+
+            def views(first, last):
+                return (
+                    grouped[:, first:last].rearrange("p n (u i) -> p n u i", u=TILES // BANK_TILES),
+                    relu[:, :, first:last].rearrange("p u n i -> p n u i"),
+                )
+
+            scalar_slots = C // 2 if e in (0, E - 1) else C
+            squared, source = views(0, scalar_slots)
+            nc.scalar.activation(squared, source, SQUARE)
+            if scalar_slots < C:
+                squared, source = views(scalar_slots, C)
+                nc.vector.tensor_tensor(squared, source, source, MULT)
+
+            h_words = h_codes_pool.tile([P, C], U32, name="h_words", align_bytes=64)
+            h_scales = h_codes_pool.tile([P, C], U8, name="h_scales", align_bytes=64)
+            nc.vector.quantize_mx(
+                out=h_words[:].bitcast(FP8X4), scales=h_scales[:], in_=grouped[:].rearrange("p n j -> p (n j)")
+            )
+            return h_words, h_scales
+
+        def layer2(e, h_words, h_scales):
+            y = y_pool.tile([P, OUT_TILES, C], F32, name="y", align_bytes=64)
+            for b in range(OUT_TILES):
+                features = slice(P * b, P * (b + 1))
+                sums = y_psum.tile([P, C], F32, name="y_sums")
+                nc.tensor.matmul_mx(
+                    out=sums[:],
+                    lhsT=w2_words[:, e, features].bitcast(FP8X4),
+                    lhsT_scale=w2_scales[:, e, features],
+                    rhs=h_words[:].bitcast(FP8X4),
+                    rhs_scale=h_scales[:],
+                    start=True,
+                    stop=True,
+                )
+                nc.scalar.copy(y[:, b], sums[:])
+            return y
+
+        def scatter(e, y):
+            slots = slice(C * e, C * (e + 1))
+            places = slots_list[:, C // LIST_ROWS * e : C // LIST_ROWS * (e + 1)]
+            for b in range(OUT_TILES):
+                nc.vector.tensor_tensor(windows[b][:].indirect(places), y[:, b], gate_sb[:, b, slots], MULT)
+
+        quantise_x(0)
+        gather_words(0)
+        quantise_x(1)
+        y = None
+        for e in range(E):
+            quantise_w1(e)
+            if e == 0:
+                gather_words(1)
+                gather_scales()
+            else:
+                scatter(e - 1, y)
+            h_words, h_scales = layer1(e)
+            if e % 2 == 0:
+                quantise_w2(e // 2)
+            y = layer2(e, h_words, h_scales)
+        scatter(E - 1, y)
+
+        for b in range(OUT_TILES):
+            nc.sync.dma_start(out[P * b : P * (b + 1), :], windows[b][:])

@@ -24,8 +24,18 @@ OUT_TILES = N // P
 LIST_ROWS = 16
 CHUNK = 512
 
-X_VECTOR = 192
-W1_VECTOR = (0, 64, 32, 48)
+X_VECTOR = (192, 192, 192, 0, 192, 352)
+W2_VECTOR = (256, 0, 0, 0)
+SQ_VECTOR = (0, 0, 0, 64)
+W1_VECTOR = (32, 32, 96, 64, 48, 48, 48, 64)
+W1_PIECES = 1
+LAG_W2 = 1
+LAG_GATE = (3, 3)
+GATHER_BUFS = 2
+SCATTER_LAG = 1
+GSLOTS = 256
+RAW_BUFS = 10
+HB = 4
 
 
 def interleave(copy, grouped, raw):
@@ -46,29 +56,25 @@ def tile_routed_moe_kernel(tc, xT, w1, w2, gate, offs, out):
     nc = tc.nc
     with ExitStack() as ctx:
         keep = ctx.enter_context(tc.tile_pool(name="keep", bufs=1))
-        raw_pool = ctx.enter_context(tc.tile_pool(name="raw_pool", bufs=11))
-        x_pool = ctx.enter_context(tc.tile_pool(name="x_pool", bufs=2))
-        w1_pool = ctx.enter_context(tc.tile_pool(name="w1_pool", bufs=2))
+        raw_pool = ctx.enter_context(tc.tile_pool(name="raw_pool", bufs=RAW_BUFS))
+        x_pool = ctx.enter_context(tc.tile_pool(name="x_pool", bufs=3))
+        w1_pool = ctx.enter_context(tc.tile_pool(name="w1_pool", bufs=3))
         w2_pool = ctx.enter_context(tc.tile_pool(name="w2_pool", bufs=2))
         relu_pool = ctx.enter_context(tc.tile_pool(name="relu_pool", bufs=2))
         h_pool = ctx.enter_context(tc.tile_pool(name="h_pool", bufs=2))
-        h_codes_pool = ctx.enter_context(tc.tile_pool(name="h_codes_pool", bufs=3))
-        y_pool = ctx.enter_context(tc.tile_pool(name="y_pool", bufs=2))
-        h_psum = ctx.enter_context(tc.psum_pool(name="h_psum", bufs=5))
-        y_psum = ctx.enter_context(tc.psum_pool(name="y_psum", bufs=3))
+        slot_pool = ctx.enter_context(tc.tile_pool(name="slot_pool", bufs=GATHER_BUFS))
+        h_psum = ctx.enter_context(tc.psum_pool(name="h_psum", bufs=HB))
+        y_psum = ctx.enter_context(tc.psum_pool(name="y_psum", bufs=8 - HB))
 
         slots_list = keep.tile([P, E * C // LIST_ROWS], U16, name="slots_list", align_bytes=64)
         words = [keep.tile([P, T], U32, name=f"words{a}", align_bytes=64) for a in range(PASSES)]
         scales = keep.tile([P, T], U8, name="scales", align_bytes=64)
         nc.gpsimd.memset(scales[:], 0)
         windows = [keep.tile([P, T], F32, name=f"window{b}", align_bytes=64) for b in range(OUT_TILES)]
-        slot_words = keep.tile([P, PASSES, E * C], U32, name="slot_words", align_bytes=64)
-        slot_scales = keep.tile([P, E * C], U8, name="slot_scales", align_bytes=64)
-        gate_sb = keep.tile([P, OUT_TILES, E * C], F32, name="gate_sb", align_bytes=64)
-        w2_words = keep.tile([P, E, N], U32, name="w2_words", align_bytes=64)
-        w2_scales = keep.tile([P, E, N], U8, name="w2_scales", align_bytes=64)
+        slot_words0 = keep.tile([P, E * C], U32, name="slot_words0", align_bytes=64)
+        gate_sb = {}
 
-        x_raw, w1_raw, w2_raw, w1_words, w1_scales = {}, {}, {}, {}, {}
+        x_raw, w1_raw, w2_raw = {}, {}, {}
 
         def load_x(a):
             rows = xT.rearrange("(a p j) n -> a p j n", p=P, j=PACK)[a]
@@ -76,26 +82,31 @@ def tile_routed_moe_kernel(tc, xT, w1, w2, gate, offs, out):
                 x_raw[a, c] = raw_pool.tile([P, PACK, CHUNK], F32, name="raw", align_bytes=64)
                 nc.sync.dma_start(x_raw[a, c][:], rows[:, :, c * CHUNK : (c + 1) * CHUNK])
 
-        def load_w1(e):
-            for a in range(PASSES):
-                w1_raw[e, a] = raw_pool.tile([P, PACK, H], F32, name="raw", align_bytes=64)
-                nc.sync.dma_start(w1_raw[e, a][:], w1[e].rearrange("(a p j) h -> a p j h", p=P, j=PACK)[a])
+        def load_w1(e, a):
+            w1_raw[e, a] = raw_pool.tile([P, PACK, H], F32, name="raw", align_bytes=64)
+            nc.sync.dma_start(w1_raw[e, a][:], w1[e].rearrange("(a p j) h -> a p j h", p=P, j=PACK)[a])
 
-        def load_w2(pair):
-            w2_raw[pair] = keep.tile([P, 2, PACK, N], F32, name=f"w2_raw{pair}", align_bytes=64)
-            for i in range(2):
-                nc.sync.dma_start(w2_raw[pair][:, i], w2[2 * pair + i].rearrange("(p j) n -> p j n", j=PACK))
+        def load_w2(e):
+            w2_raw[e] = keep.tile([P, PACK, N], F32, name=f"w2_raw{e}", align_bytes=64)
+            nc.sync.dma_start(w2_raw[e][:], w2[e].rearrange("(p j) n -> p j n", j=PACK))
 
-        nc.sync.dma_start(slots_list[:], offs)
+        def load_gate(e, b):
+            gate_sb[e, b] = keep.tile([P, C], F32, name=f"gate_sb{e}_{b}", align_bytes=64)
+            nc.sync.dma_start(gate_sb[e, b][:], gate[P * b : P * (b + 1), C * e : C * (e + 1)])
+
         load_x(0)
+        nc.sync.dma_start(slots_list[:], offs)
         load_x(1)
-        load_w1(0)
-        load_w2(0)
-        load_w1(1)
-        load_w1(2)
-        nc.sync.dma_start(gate_sb[:], gate.rearrange("(b p) j -> p b j", p=P))
-        load_w1(3)
-        load_w2(1)
+        pieces = E * PASSES
+        for step in range(pieces + max(LAG_W2, *LAG_GATE)):
+            if step < pieces:
+                load_w1(step // PASSES, step % PASSES)
+            for e in range(E):
+                if step == PASSES * e + 1 + LAG_W2:
+                    load_w2(e)
+                for b in range(OUT_TILES):
+                    if step == PASSES * e + 1 + LAG_GATE[b]:
+                        load_gate(e, b)
 
         for b in range(OUT_TILES):
             nc.vector.memset(windows[b][:], 0.0)
@@ -104,8 +115,10 @@ def tile_routed_moe_kernel(tc, xT, w1, w2, gate, offs, out):
             for c in range(T // CHUNK):
                 grouped = x_pool.tile([P, CHUNK, PACK], BF16, name="x_grouped", align_bytes=64)
                 raw = x_raw[a, c]
-                interleave(nc.vector.tensor_copy, grouped[:, :X_VECTOR], raw[:, :, :X_VECTOR])
-                interleave(nc.scalar.copy, grouped[:, X_VECTOR:], raw[:, :, X_VECTOR:])
+                vector = X_VECTOR[a * (T // CHUNK) + c]
+                if vector > 0:
+                    interleave(nc.vector.tensor_copy, grouped[:, :vector], raw[:, :, :vector])
+                interleave(nc.scalar.copy, grouped[:, vector:], raw[:, :, vector:])
                 tokens = slice(c * CHUNK, (c + 1) * CHUNK)
                 nc.vector.quantize_mx(
                     out=words[a][:, tokens].bitcast(FP8X4),
@@ -113,43 +126,52 @@ def tile_routed_moe_kernel(tc, xT, w1, w2, gate, offs, out):
                     in_=grouped[:].rearrange("p c j -> p (c j)"),
                 )
 
-        def gather_words(a):
-            nc.vector.tensor_copy(slot_words[:, a, :], words[a][:].indirect(slots_list[:]))
+        def places(first, last):
+            return slots_list[:, first // LIST_ROWS : last // LIST_ROWS]
 
-        def gather_scales():
-            nc.vector.tensor_copy(slot_scales[:], scales[:].indirect(slots_list[:]))
+        def gather_pass1(first):
+            slot_words1 = slot_pool.tile([P, GSLOTS], U32, name="slot_words1", align_bytes=64)
+            slot_scales = slot_pool.tile([P, GSLOTS], U8, name="slot_scales", align_bytes=64)
+            nc.vector.tensor_copy(slot_words1[:], words[1][:].indirect(places(first, first + GSLOTS)))
+            nc.vector.tensor_copy(slot_scales[:], scales[:].indirect(places(first, first + GSLOTS)))
+            return slot_words1, slot_scales
 
         def quantise_w1(e):
-            w1_words[e] = keep.tile([P, PASSES, H], U32, name=f"w1_words{e}", align_bytes=64)
-            w1_scales[e] = keep.tile([P, PASSES, H], U8, name=f"w1_scales{e}", align_bytes=64)
-            at_once = PASSES if e == 0 else 1
-            vector = W1_VECTOR[e]
-            for a0 in range(0, PASSES, at_once):
-                grouped = w1_pool.tile([P, at_once, H, PACK], BF16, name="w1_grouped", align_bytes=64)
-                for i in range(at_once):
-                    raw = w1_raw[e, a0 + i][:]
-                    if vector > 0:
-                        interleave_w1(nc.vector.tensor_copy, grouped[:, i], raw, 0, vector)
-                    interleave_w1(nc.scalar.copy, grouped[:, i], raw, vector, P)
+            w1_words = keep.tile([P, PASSES, H], U32, name=f"w1_words{e}", align_bytes=64)
+            w1_scales = keep.tile([P, PASSES, H], U8, name=f"w1_scales{e}", align_bytes=64)
+            for a in range(PASSES):
+                vector = W1_VECTOR[PASSES * e + a]
+                grouped = w1_pool.tile([P, H, PACK], BF16, name="w1_grouped", align_bytes=64)
+                raw = w1_raw[e, a][:]
+                if vector > 0:
+                    interleave_w1(nc.vector.tensor_copy, grouped[:], raw, 0, vector)
+                piece = (P - vector) // W1_PIECES
+                for i in range(W1_PIECES if vector < P else 0):
+                    interleave_w1(nc.scalar.copy, grouped[:], raw, vector + i * piece, vector + (i + 1) * piece)
                 nc.vector.quantize_mx(
-                    out=w1_words[e][:, a0 : a0 + at_once].rearrange("p a h -> p (a h)").bitcast(FP8X4),
-                    scales=w1_scales[e][:, a0 : a0 + at_once].rearrange("p a h -> p (a h)"),
-                    in_=grouped[:].rearrange("p a h j -> p (a h j)"),
+                    out=w1_words[:, a].bitcast(FP8X4),
+                    scales=w1_scales[:, a],
+                    in_=grouped[:].rearrange("p h j -> p (h j)"),
                 )
+            return w1_words, w1_scales
 
-        def quantise_w2(pair):
-            grouped = w2_pool.tile([P, 2, N, PACK], BF16, name="w2_grouped", align_bytes=64)
-            for i in range(2):
-                interleave(nc.scalar.copy, grouped[:, i], w2_raw[pair][:, i])
-            experts = slice(2 * pair, 2 * pair + 2)
+        def quantise_w2(e):
+            w2_words = keep.tile([P, N], U32, name=f"w2_words{e}", align_bytes=64)
+            w2_scales = keep.tile([P, N], U8, name=f"w2_scales{e}", align_bytes=64)
+            grouped = w2_pool.tile([P, N, PACK], BF16, name="w2_grouped", align_bytes=64)
+            vector = W2_VECTOR[e]
+            if vector > 0:
+                interleave(nc.vector.tensor_copy, grouped[:, :vector], w2_raw[e][:, :, :vector])
+            if vector < N:
+                interleave(nc.scalar.copy, grouped[:, vector:], w2_raw[e][:, :, vector:])
             nc.vector.quantize_mx(
-                out=w2_words[:, experts].rearrange("p e n -> p (e n)").bitcast(FP8X4),
-                scales=w2_scales[:, experts].rearrange("p e n -> p (e n)"),
-                in_=grouped[:].rearrange("p e n j -> p (e n j)"),
+                out=w2_words[:].bitcast(FP8X4), scales=w2_scales[:], in_=grouped[:].rearrange("p n j -> p (n j)")
             )
+            return w2_words, w2_scales
 
-        def layer1(e):
-            slots = slice(C * e, C * (e + 1))
+        def layer1(e, w1_words, w1_scales, slot_words1, slot_scales):
+            slots = slice(C * e % GSLOTS, C * e % GSLOTS + C)
+            slot_words = (slot_words0[:, C * e : C * (e + 1)], slot_words1[:, slots])
             relu = relu_pool.tile([P, TILES // BANK_TILES, C, BANK_TILES], F32, name="relu", align_bytes=64)
             for u in range(TILES // BANK_TILES):
                 sums = h_psum.tile([P, BANK_TILES, C], F32, name="h_sums")
@@ -159,9 +181,9 @@ def tile_routed_moe_kernel(tc, xT, w1, w2, gate, offs, out):
                     for a in range(PASSES):
                         nc.tensor.matmul_mx(
                             out=sums[:, i],
-                            lhsT=w1_words[e][:, a, columns].bitcast(FP8X4),
-                            lhsT_scale=w1_scales[e][:, a, columns],
-                            rhs=slot_words[:, a, slots].bitcast(FP8X4),
+                            lhsT=w1_words[:, a, columns].bitcast(FP8X4),
+                            lhsT_scale=w1_scales[:, a, columns],
+                            rhs=slot_words[a].bitcast(FP8X4),
                             rhs_scale=slot_scales[4 * a : P, slots],
                             start=(a == 0),
                             stop=(a == PASSES - 1),
@@ -176,29 +198,29 @@ def tile_routed_moe_kernel(tc, xT, w1, w2, gate, offs, out):
                     relu[:, :, first:last].rearrange("p u n i -> p n u i"),
                 )
 
-            scalar_slots = C // 2 if e in (0, E - 1) else C
+            scalar_slots = C - SQ_VECTOR[e]
             squared, source = views(0, scalar_slots)
             nc.scalar.activation(squared, source, SQUARE)
             if scalar_slots < C:
                 squared, source = views(scalar_slots, C)
                 nc.vector.tensor_tensor(squared, source, source, MULT)
 
-            h_words = h_codes_pool.tile([P, C], U32, name="h_words", align_bytes=64)
-            h_scales = h_codes_pool.tile([P, C], U8, name="h_scales", align_bytes=64)
+            h_words = keep.tile([P, C], U32, name=f"h_words{e}", align_bytes=64)
+            h_scales = keep.tile([P, C], U8, name=f"h_scales{e}", align_bytes=64)
             nc.vector.quantize_mx(
                 out=h_words[:].bitcast(FP8X4), scales=h_scales[:], in_=grouped[:].rearrange("p n j -> p (n j)")
             )
             return h_words, h_scales
 
-        def layer2(e, h_words, h_scales):
-            y = y_pool.tile([P, OUT_TILES, C], F32, name="y", align_bytes=64)
+        def layer2(e, w2_words, w2_scales, h_words, h_scales):
+            y = keep.tile([P, OUT_TILES, C], F32, name=f"y{e}", align_bytes=64)
             for b in range(OUT_TILES):
                 features = slice(P * b, P * (b + 1))
                 sums = y_psum.tile([P, C], F32, name="y_sums")
                 nc.tensor.matmul_mx(
                     out=sums[:],
-                    lhsT=w2_words[:, e, features].bitcast(FP8X4),
-                    lhsT_scale=w2_scales[:, e, features],
+                    lhsT=w2_words[:, features].bitcast(FP8X4),
+                    lhsT_scale=w2_scales[:, features],
                     rhs=h_words[:].bitcast(FP8X4),
                     rhs_scale=h_scales[:],
                     start=True,
@@ -208,27 +230,25 @@ def tile_routed_moe_kernel(tc, xT, w1, w2, gate, offs, out):
             return y
 
         def scatter(e, y):
-            slots = slice(C * e, C * (e + 1))
-            places = slots_list[:, C // LIST_ROWS * e : C // LIST_ROWS * (e + 1)]
             for b in range(OUT_TILES):
-                nc.vector.tensor_tensor(windows[b][:].indirect(places), y[:, b], gate_sb[:, b, slots], MULT)
+                nc.vector.tensor_tensor(
+                    windows[b][:].indirect(places(C * e, C * (e + 1))), y[:, b], gate_sb[e, b][:], MULT
+                )
 
         quantise_x(0)
-        gather_words(0)
         quantise_x(1)
-        y = None
-        for e in range(E):
-            quantise_w1(e)
-            if e == 0:
-                gather_words(1)
-                gather_scales()
-            else:
-                scatter(e - 1, y)
-            h_words, h_scales = layer1(e)
-            if e % 2 == 0:
-                quantise_w2(e // 2)
-            y = layer2(e, h_words, h_scales)
-        scatter(E - 1, y)
+        nc.vector.tensor_copy(slot_words0[:], words[0][:].indirect(slots_list[:]))
+        ys = []
+        for e in range(E + SCATTER_LAG):
+            if e < E:
+                if C * e % GSLOTS == 0:
+                    gathered = gather_pass1(C * e)
+                w1_codes = quantise_w1(e)
+                h_codes = layer1(e, *w1_codes, *gathered)
+                w2_codes = quantise_w2(e)
+                ys.append(layer2(e, *w2_codes, *h_codes))
+            if 0 <= e - SCATTER_LAG < E:
+                scatter(e - SCATTER_LAG, ys[e - SCATTER_LAG])
 
         for b in range(OUT_TILES):
             nc.sync.dma_start(out[P * b : P * (b + 1), :], windows[b][:])

@@ -24,17 +24,25 @@ OUT_TILES = N // P
 LIST_ROWS = 16
 CHUNK = 512
 
-X_VECTOR = (192, 192, 192, 0, 192, 352)
-W2_VECTOR = (256, 0, 0, 0)
-SQ_VECTOR = (0, 0, 0, 64)
-W1_VECTOR = (32, 32, 96, 64, 48, 48, 48, 64)
+X_VECTOR = ((192, 192, 192), (0, 192, 256))
+W2_VECTOR = (256, 256, 256, 0)
+SQ_VECTOR = (0, 0, 0, 128)
+W1_VECTOR = (0, 0, 96, 32, 96, 32, 96, 32)
 W1_PIECES = 1
-LAG_W2 = 1
-LAG_GATE = (3, 3)
-GATHER_BUFS = 2
-SCATTER_LAG = 1
-GSLOTS = 256
-RAW_BUFS = 10
+W2_STEP = (1, 2)
+GATE_STEP = (5, 5, 2)
+GATHER_BUFS = 4
+SCATTER_LAG = 4
+X_LOADS = ((512, 512, 512), (512, 512, 512))
+X_STEPS = ((512, 512, 512), (512, 512, 512))
+RELU_LAG = 2
+SQUARE_LAG = 4
+Y_LAG = 4
+RELU_HOST = True
+SQUARE_HOST = False
+Y_HOST = True
+GCUTS = (0, 256, 1024)
+RAW_BUFS = 11
 HB = 4
 
 
@@ -72,15 +80,20 @@ def tile_routed_moe_kernel(tc, xT, w1, w2, gate, offs, out):
         nc.gpsimd.memset(scales[:], 0)
         windows = [keep.tile([P, T], F32, name=f"window{b}", align_bytes=64) for b in range(OUT_TILES)]
         slot_words0 = keep.tile([P, E * C], U32, name="slot_words0", align_bytes=64)
-        gate_sb = {}
+        gate_sb, w1_words, w1_scales = {}, {}, {}
 
         x_raw, w1_raw, w2_raw = {}, {}, {}
 
         def load_x(a):
             rows = xT.rearrange("(a p j) n -> a p j n", p=P, j=PACK)[a]
-            for c in range(T // CHUNK):
-                x_raw[a, c] = raw_pool.tile([P, PACK, CHUNK], F32, name="raw", align_bytes=64)
-                nc.sync.dma_start(x_raw[a, c][:], rows[:, :, c * CHUNK : (c + 1) * CHUNK])
+            first = 0
+            for width in X_LOADS[a]:
+                tag, bufs = ("raw", RAW_BUFS) if width <= CHUNK else (f"x_raw{a}", 1)
+                raw = raw_pool.tile([P, PACK, width], F32, name=tag, align_bytes=64, bufs=bufs)
+                nc.sync.dma_start(raw[:], rows[:, :, first : first + width])
+                for token in range(first, first + width, P):
+                    x_raw[a, token] = (raw, first)
+                first += width
 
         def load_w1(e, a):
             w1_raw[e, a] = raw_pool.tile([P, PACK, H], F32, name="raw", align_bytes=64)
@@ -98,28 +111,33 @@ def tile_routed_moe_kernel(tc, xT, w1, w2, gate, offs, out):
         nc.sync.dma_start(slots_list[:], offs)
         load_x(1)
         pieces = E * PASSES
-        for step in range(pieces + max(LAG_W2, *LAG_GATE)):
+        for step in range(2 * pieces):
             if step < pieces:
                 load_w1(step // PASSES, step % PASSES)
             for e in range(E):
-                if step == PASSES * e + 1 + LAG_W2:
+                if step == W2_STEP[0] + W2_STEP[1] * e:
                     load_w2(e)
+            for e in range(E):
                 for b in range(OUT_TILES):
-                    if step == PASSES * e + 1 + LAG_GATE[b]:
+                    if step == GATE_STEP[b] + GATE_STEP[2] * e:
                         load_gate(e, b)
 
         for b in range(OUT_TILES):
             nc.vector.memset(windows[b][:], 0.0)
 
         def quantise_x(a):
-            for c in range(T // CHUNK):
-                grouped = x_pool.tile([P, CHUNK, PACK], BF16, name="x_grouped", align_bytes=64)
-                raw = x_raw[a, c]
-                vector = X_VECTOR[a * (T // CHUNK) + c]
+            first = 0
+            for c, width in enumerate(X_STEPS[a]):
+                grouped = x_pool.tile([P, width, PACK], BF16, name="x_grouped", align_bytes=64)
+                tile, start = x_raw[a, first]
+                raw = tile[:, :, first - start : first - start + width]
+                vector = X_VECTOR[a][c]
                 if vector > 0:
                     interleave(nc.vector.tensor_copy, grouped[:, :vector], raw[:, :, :vector])
-                interleave(nc.scalar.copy, grouped[:, vector:], raw[:, :, vector:])
-                tokens = slice(c * CHUNK, (c + 1) * CHUNK)
+                if vector < width:
+                    interleave(nc.scalar.copy, grouped[:, vector:], raw[:, :, vector:])
+                tokens = slice(first, first + width)
+                first += width
                 nc.vector.quantize_mx(
                     out=words[a][:, tokens].bitcast(FP8X4),
                     scales=scales[4 * a : P, tokens],
@@ -129,31 +147,33 @@ def tile_routed_moe_kernel(tc, xT, w1, w2, gate, offs, out):
         def places(first, last):
             return slots_list[:, first // LIST_ROWS : last // LIST_ROWS]
 
-        def gather_pass1(first):
-            slot_words1 = slot_pool.tile([P, GSLOTS], U32, name="slot_words1", align_bytes=64)
-            slot_scales = slot_pool.tile([P, GSLOTS], U8, name="slot_scales", align_bytes=64)
-            nc.vector.tensor_copy(slot_words1[:], words[1][:].indirect(places(first, first + GSLOTS)))
-            nc.vector.tensor_copy(slot_scales[:], scales[:].indirect(places(first, first + GSLOTS)))
-            return slot_words1, slot_scales
+        def gather_pass1(first, last):
+            slot_words1 = slot_pool.tile([P, last - first], U32, name="slot_words1", align_bytes=64)
+            slot_scales = slot_pool.tile([P, last - first], U8, name="slot_scales", align_bytes=64)
+            nc.vector.tensor_copy(slot_words1[:], words[1][:].indirect(places(first, last)))
+            nc.vector.tensor_copy(slot_scales[:], scales[:].indirect(places(first, last)))
+            return slot_words1, slot_scales, first
 
-        def quantise_w1(e):
-            w1_words = keep.tile([P, PASSES, H], U32, name=f"w1_words{e}", align_bytes=64)
-            w1_scales = keep.tile([P, PASSES, H], U8, name=f"w1_scales{e}", align_bytes=64)
-            for a in range(PASSES):
-                vector = W1_VECTOR[PASSES * e + a]
-                grouped = w1_pool.tile([P, H, PACK], BF16, name="w1_grouped", align_bytes=64)
-                raw = w1_raw[e, a][:]
-                if vector > 0:
-                    interleave_w1(nc.vector.tensor_copy, grouped[:], raw, 0, vector)
-                piece = (P - vector) // W1_PIECES
-                for i in range(W1_PIECES if vector < P else 0):
-                    interleave_w1(nc.scalar.copy, grouped[:], raw, vector + i * piece, vector + (i + 1) * piece)
-                nc.vector.quantize_mx(
-                    out=w1_words[:, a].bitcast(FP8X4),
-                    scales=w1_scales[:, a],
-                    in_=grouped[:].rearrange("p h j -> p (h j)"),
-                )
-            return w1_words, w1_scales
+        def quantise_w1(e, a):
+            if a == 0:
+                w1_words[e] = keep.tile([P, PASSES, H], U32, name=f"w1_words{e}", align_bytes=64)
+                w1_scales[e] = keep.tile([P, PASSES, H], U8, name=f"w1_scales{e}", align_bytes=64)
+            vector = W1_VECTOR[PASSES * e + a]
+            raw = w1_raw[e, a][:]
+            grouped = w1_pool.tile([P, H, PACK], BF16, name="w1_grouped", align_bytes=64)
+            if vector > 0:
+                interleave_w1(nc.vector.tensor_copy, grouped[:], raw, 0, vector)
+            piece = (P - vector) // W1_PIECES
+            for i in range(W1_PIECES if vector < P else 0):
+                interleave_w1(nc.scalar.copy, grouped[:], raw, vector + i * piece, vector + (i + 1) * piece)
+            nc.vector.quantize_mx(
+                out=w1_words[e][:, a].bitcast(FP8X4),
+                scales=w1_scales[e][:, a],
+                in_=grouped[:].rearrange("p h j -> p (h j)"),
+            )
+
+        def spent(step):
+            return w1_raw[step // PASSES, step % PASSES][:].rearrange("p j h -> p (j h)")
 
         def quantise_w2(e):
             w2_words = keep.tile([P, N], U32, name=f"w2_words{e}", align_bytes=64)
@@ -169,51 +189,60 @@ def tile_routed_moe_kernel(tc, xT, w1, w2, gate, offs, out):
             )
             return w2_words, w2_scales
 
-        def layer1(e, w1_words, w1_scales, slot_words1, slot_scales):
-            slots = slice(C * e % GSLOTS, C * e % GSLOTS + C)
+        def layer1(e, slot_words1, slot_scales, first):
+            slots = slice(C * e - first, C * (e + 1) - first)
             slot_words = (slot_words0[:, C * e : C * (e + 1)], slot_words1[:, slots])
-            relu = relu_pool.tile([P, TILES // BANK_TILES, C, BANK_TILES], F32, name="relu", align_bytes=64)
+            banks = []
             for u in range(TILES // BANK_TILES):
                 sums = h_psum.tile([P, BANK_TILES, C], F32, name="h_sums")
+                banks.append(sums)
                 for i in range(BANK_TILES):
                     t = BANK_TILES * u + i
                     columns = slice(P * t, P * (t + 1))
                     for a in range(PASSES):
                         nc.tensor.matmul_mx(
                             out=sums[:, i],
-                            lhsT=w1_words[:, a, columns].bitcast(FP8X4),
-                            lhsT_scale=w1_scales[:, a, columns],
+                            lhsT=w1_words[e][:, a, columns].bitcast(FP8X4),
+                            lhsT_scale=w1_scales[e][:, a, columns],
                             rhs=slot_words[a].bitcast(FP8X4),
                             rhs_scale=slot_scales[4 * a : P, slots],
                             start=(a == 0),
                             stop=(a == PASSES - 1),
                         )
-                nc.scalar.activation(relu[:, u], sums[:].rearrange("p i n -> p n i"), RELU)
+            return banks
 
-            grouped = h_pool.tile([P, C, PACK], BF16, name="h_grouped", align_bytes=64)
+        def rectify(e, step, banks):
+            if RELU_HOST and step < pieces and RELU_LAG > 0:
+                flat = spent(step)[:, 2 * H :]
+            else:
+                flat = relu_pool.tile([P, TILES * C], F32, name="relu", align_bytes=64)[:]
+            relu = flat.rearrange("p (u n i) -> p u n i", u=TILES // BANK_TILES, i=BANK_TILES)
+            for u in range(TILES // BANK_TILES):
+                nc.scalar.activation(relu[:, u], banks[u][:].rearrange("p i n -> p n i"), RELU)
+            return relu
 
-            def views(first, last):
-                return (
-                    grouped[:, first:last].rearrange("p n (u i) -> p n u i", u=TILES // BANK_TILES),
-                    relu[:, :, first:last].rearrange("p u n i -> p n u i"),
-                )
-
+        def square(e, step, relu):
+            if SQUARE_HOST and step < pieces and SQUARE_LAG > 0:
+                flat = spent(step)[:, H : 2 * H].bitcast(BF16)
+            else:
+                flat = h_pool.tile([P, C * PACK], BF16, name="h_grouped", align_bytes=64)[:]
+            grouped = flat.rearrange("p (n u i) -> p n u i", u=TILES // BANK_TILES, i=BANK_TILES)
+            source = relu.rearrange("p u n i -> p n u i")
             scalar_slots = C - SQ_VECTOR[e]
-            squared, source = views(0, scalar_slots)
-            nc.scalar.activation(squared, source, SQUARE)
+            nc.scalar.activation(grouped[:, :scalar_slots], source[:, :scalar_slots], SQUARE)
             if scalar_slots < C:
-                squared, source = views(scalar_slots, C)
-                nc.vector.tensor_tensor(squared, source, source, MULT)
-
+                nc.vector.tensor_tensor(grouped[:, scalar_slots:], source[:, scalar_slots:], source[:, scalar_slots:], MULT)
             h_words = keep.tile([P, C], U32, name=f"h_words{e}", align_bytes=64)
             h_scales = keep.tile([P, C], U8, name=f"h_scales{e}", align_bytes=64)
-            nc.vector.quantize_mx(
-                out=h_words[:].bitcast(FP8X4), scales=h_scales[:], in_=grouped[:].rearrange("p n j -> p (n j)")
-            )
+            nc.vector.quantize_mx(out=h_words[:].bitcast(FP8X4), scales=h_scales[:], in_=flat)
             return h_words, h_scales
 
-        def layer2(e, w2_words, w2_scales, h_words, h_scales):
-            y = keep.tile([P, OUT_TILES, C], F32, name=f"y{e}", align_bytes=64)
+        def layer2(e, step, w2_words, w2_scales, h_words, h_scales):
+            if Y_HOST and step < pieces and Y_LAG > 0:
+                flat = spent(step)[:, :H]
+            else:
+                flat = keep.tile([P, OUT_TILES * C], F32, name=f"y{e}", align_bytes=64)[:]
+            y = flat.rearrange("p (b c) -> p b c", b=OUT_TILES)
             for b in range(OUT_TILES):
                 features = slice(P * b, P * (b + 1))
                 sums = y_psum.tile([P, C], F32, name="y_sums")
@@ -238,17 +267,25 @@ def tile_routed_moe_kernel(tc, xT, w1, w2, gate, offs, out):
         quantise_x(0)
         quantise_x(1)
         nc.vector.tensor_copy(slot_words0[:], words[0][:].indirect(slots_list[:]))
-        ys = []
-        for e in range(E + SCATTER_LAG):
-            if e < E:
-                if C * e % GSLOTS == 0:
-                    gathered = gather_pass1(C * e)
-                w1_codes = quantise_w1(e)
-                h_codes = layer1(e, *w1_codes, *gathered)
-                w2_codes = quantise_w2(e)
-                ys.append(layer2(e, *w2_codes, *h_codes))
-            if 0 <= e - SCATTER_LAG < E:
-                scatter(e - SCATTER_LAG, ys[e - SCATTER_LAG])
+        stage = {}
+        for step in range(2 * pieces):
+            if step < pieces:
+                e, a = divmod(step, PASSES)
+                if a == 0 and C * e in GCUTS:
+                    gathered = gather_pass1(C * e, GCUTS[GCUTS.index(C * e) + 1])
+                quantise_w1(e, a)
+                if a == PASSES - 1:
+                    stage[e] = layer1(e, *gathered)
+            for e in range(E):
+                age = step - (PASSES * e + 1)
+                if age == RELU_LAG:
+                    stage[e] = rectify(e, step, stage[e])
+                if age == SQUARE_LAG:
+                    stage[e] = square(e, step, stage[e])
+                if age == Y_LAG:
+                    stage[e] = layer2(e, step, *quantise_w2(e), *stage[e])
+                if age == SCATTER_LAG:
+                    scatter(e, stage[e])
 
         for b in range(OUT_TILES):
             nc.sync.dma_start(out[P * b : P * (b + 1), :], windows[b][:])

@@ -24,39 +24,39 @@ OUT_TILES = N // P
 LIST_ROWS = 16
 CHUNK = 512
 
-X_VECTOR = ((192, 192, 192), (0, 192, 256))
-W2_VECTOR = (256, 256, 256, 0)
-SQ_VECTOR = (0, 0, 0, 128)
-W1_VECTOR = (0, 0, 96, 32, 96, 32, 96, 32)
+X_VECTOR = ((256, 256, 256), (0, 256, 256))
+W2_VECTOR = (256, 256, 256, 256)
+SQ_VECTOR = (0, 0, 0, 0)
+W1_VECTOR = (0, 0, 64, 64, 64, 64, 64, 0)
 W1_PIECES = 1
-W2_STEP = (1, 2)
-GATE_STEP = (5, 5, 2)
+W2_STEP = (3, 5, 7, 8)
+GATE_STEP = ((5, 7, 9, 11), (6, 8, 10, 12))
 GATHER_BUFS = 4
-SCATTER_LAG = 4
+SCATTER_LAG = (4, 4, 4, 4)
 X_LOADS = ((512, 512, 512), (512, 512, 512))
 X_STEPS = ((512, 512, 512), (512, 512, 512))
-RELU_LAG = 2
-SQUARE_LAG = 4
-Y_LAG = 4
+RELU_LAG = (2, 2, 2, 2)
+SQUARE_LAG = (4, 4, 4, 4)
+Y_LAG = (4, 4, 4, 4)
 RELU_HOST = True
 SQUARE_HOST = False
 Y_HOST = True
-GCUTS = (0, 256, 1024)
+GCUTS = (0, 1024)
 RAW_BUFS = 11
 HB = 4
 
 
 def interleave(copy, grouped, raw):
     copy(
-        grouped.rearrange("p (c i) j -> p c j i", i=4),
-        raw.rearrange("p j (c i) -> p c j i", i=4),
+        grouped.rearrange("p (c i) j -> p c j i", i=2),
+        raw.rearrange("p j (c i) -> p c j i", i=2),
     )
 
 
 def interleave_w1(copy, grouped, raw, first, last):
     copy(
-        grouped.rearrange("p (t m) j -> p m j t", t=TILES)[:, first:last],
-        raw.rearrange("p j (m t) -> p m j t", t=TILES)[:, first:last],
+        grouped.rearrange("p (t r s) j -> p r t j s", t=TILES, s=2)[:, first // 2 : last // 2],
+        raw.rearrange("p j (r t s) -> p r t j s", t=TILES, s=2)[:, first // 2 : last // 2],
     )
 
 
@@ -101,7 +101,9 @@ def tile_routed_moe_kernel(tc, xT, w1, w2, gate, offs, out):
 
         def load_w2(e):
             w2_raw[e] = keep.tile([P, PACK, N], F32, name=f"w2_raw{e}", align_bytes=64)
-            nc.sync.dma_start(w2_raw[e][:], w2[e].rearrange("(p j) n -> p j n", j=PACK))
+            rows = w2[e].rearrange("(r t s) n -> s r t n", t=PACK, s=2)
+            for s in range(2):
+                nc.sync.dma_start(w2_raw[e][s:P:2], rows[s])
 
         def load_gate(e, b):
             gate_sb[e, b] = keep.tile([P, C], F32, name=f"gate_sb{e}_{b}", align_bytes=64)
@@ -115,11 +117,11 @@ def tile_routed_moe_kernel(tc, xT, w1, w2, gate, offs, out):
             if step < pieces:
                 load_w1(step // PASSES, step % PASSES)
             for e in range(E):
-                if step == W2_STEP[0] + W2_STEP[1] * e:
+                if step == W2_STEP[e]:
                     load_w2(e)
             for e in range(E):
                 for b in range(OUT_TILES):
-                    if step == GATE_STEP[b] + GATE_STEP[2] * e:
+                    if step == GATE_STEP[b][e]:
                         load_gate(e, b)
 
         for b in range(OUT_TILES):
@@ -212,7 +214,7 @@ def tile_routed_moe_kernel(tc, xT, w1, w2, gate, offs, out):
             return banks
 
         def rectify(e, step, banks):
-            if RELU_HOST and step < pieces and RELU_LAG > 0:
+            if RELU_HOST and step < pieces and RELU_LAG[e] > 0:
                 flat = spent(step)[:, 2 * H :]
             else:
                 flat = relu_pool.tile([P, TILES * C], F32, name="relu", align_bytes=64)[:]
@@ -222,7 +224,7 @@ def tile_routed_moe_kernel(tc, xT, w1, w2, gate, offs, out):
             return relu
 
         def square(e, step, relu):
-            if SQUARE_HOST and step < pieces and SQUARE_LAG > 0:
+            if SQUARE_HOST and step < pieces and SQUARE_LAG[e] > 0:
                 flat = spent(step)[:, H : 2 * H].bitcast(BF16)
             else:
                 flat = h_pool.tile([P, C * PACK], BF16, name="h_grouped", align_bytes=64)[:]
@@ -238,7 +240,7 @@ def tile_routed_moe_kernel(tc, xT, w1, w2, gate, offs, out):
             return h_words, h_scales
 
         def layer2(e, step, w2_words, w2_scales, h_words, h_scales):
-            if Y_HOST and step < pieces and Y_LAG > 0:
+            if Y_HOST and step < pieces and Y_LAG[e] > 0:
                 flat = spent(step)[:, :H]
             else:
                 flat = keep.tile([P, OUT_TILES * C], F32, name=f"y{e}", align_bytes=64)[:]
@@ -278,13 +280,13 @@ def tile_routed_moe_kernel(tc, xT, w1, w2, gate, offs, out):
                     stage[e] = layer1(e, *gathered)
             for e in range(E):
                 age = step - (PASSES * e + 1)
-                if age == RELU_LAG:
+                if age == RELU_LAG[e]:
                     stage[e] = rectify(e, step, stage[e])
-                if age == SQUARE_LAG:
+                if age == SQUARE_LAG[e]:
                     stage[e] = square(e, step, stage[e])
-                if age == Y_LAG:
+                if age == Y_LAG[e]:
                     stage[e] = layer2(e, step, *quantise_w2(e), *stage[e])
-                if age == SCATTER_LAG:
+                if age == SCATTER_LAG[e]:
                     scatter(e, stage[e])
 
         for b in range(OUT_TILES):

@@ -17,46 +17,33 @@ SQUARE = mybir.ActivationFunctionType.Square
 
 P = 128
 PACK = 4
+PAIR = 2
 PASSES = K // (P * PACK)
+HALVES = E * PASSES
 TILES = H // P
 BANK_TILES = 2
+BANKS = TILES // BANK_TILES
 OUT_TILES = N // P
 LIST_ROWS = 16
+SCALE_ROWS = 4
 CHUNK = 512
+LONG = 2 * CHUNK
 
-X_VECTOR = ((256, 256, 256), (0, 256, 256))
-W2_VECTOR = (256, 256, 256, 256)
-SQ_VECTOR = (0, 0, 0, 0)
-W1_VECTOR = (0, 0, 64, 64, 64, 64, 64, 0)
-W1_PIECES = 1
-W2_STEP = (3, 5, 7, 8)
-GATE_STEP = ((5, 7, 9, 11), (6, 8, 10, 12))
-GATHER_BUFS = 4
-SCATTER_LAG = (4, 4, 4, 4)
-X_LOADS = ((512, 512, 512), (512, 512, 512))
-X_STEPS = ((512, 512, 512), (512, 512, 512))
-RELU_LAG = (2, 2, 2, 2)
-SQUARE_LAG = (4, 4, 4, 4)
-Y_LAG = (4, 4, 4, 4)
-RELU_HOST = True
-SQUARE_HOST = False
-Y_HOST = True
-GCUTS = (0, 1024)
-RAW_BUFS = 11
-HB = 4
+W2_LAG = 2
+GATE_LAG = 4
 
 
 def interleave(copy, grouped, raw):
     copy(
-        grouped.rearrange("p (c i) j -> p c j i", i=2),
-        raw.rearrange("p j (c i) -> p c j i", i=2),
+        grouped.rearrange("p (c i) j -> p c j i", i=PAIR),
+        raw.rearrange("p j (c i) -> p c j i", i=PAIR),
     )
 
 
-def interleave_w1(copy, grouped, raw, first, last):
+def interleave_w1(copy, grouped, raw, groups):
     copy(
-        grouped.rearrange("p (t r s) j -> p r t j s", t=TILES, s=2)[:, first // 2 : last // 2],
-        raw.rearrange("p j (r t s) -> p r t j s", t=TILES, s=2)[:, first // 2 : last // 2],
+        grouped.rearrange("p (t r s) j -> p r t j s", t=TILES, s=PAIR)[:, groups],
+        raw.rearrange("p j (r t s) -> p r t j s", t=TILES, s=PAIR)[:, groups],
     )
 
 
@@ -64,36 +51,31 @@ def tile_routed_moe_kernel(tc, xT, w1, w2, gate, offs, out):
     nc = tc.nc
     with ExitStack() as ctx:
         keep = ctx.enter_context(tc.tile_pool(name="keep", bufs=1))
-        raw_pool = ctx.enter_context(tc.tile_pool(name="raw_pool", bufs=RAW_BUFS))
+        raw_pool = ctx.enter_context(tc.tile_pool(name="raw_pool", bufs=8))
         x_pool = ctx.enter_context(tc.tile_pool(name="x_pool", bufs=3))
         w1_pool = ctx.enter_context(tc.tile_pool(name="w1_pool", bufs=3))
         w2_pool = ctx.enter_context(tc.tile_pool(name="w2_pool", bufs=2))
-        relu_pool = ctx.enter_context(tc.tile_pool(name="relu_pool", bufs=2))
         h_pool = ctx.enter_context(tc.tile_pool(name="h_pool", bufs=2))
-        slot_pool = ctx.enter_context(tc.tile_pool(name="slot_pool", bufs=GATHER_BUFS))
-        h_psum = ctx.enter_context(tc.psum_pool(name="h_psum", bufs=HB))
-        y_psum = ctx.enter_context(tc.psum_pool(name="y_psum", bufs=8 - HB))
+        h_psum = ctx.enter_context(tc.psum_pool(name="h_psum", bufs=2 * BANKS))
+        y_psum = ctx.enter_context(tc.psum_pool(name="y_psum", bufs=2 * OUT_TILES))
 
         slots_list = keep.tile([P, E * C // LIST_ROWS], U16, name="slots_list", align_bytes=64)
         words = [keep.tile([P, T], U32, name=f"words{a}", align_bytes=64) for a in range(PASSES)]
         scales = keep.tile([P, T], U8, name="scales", align_bytes=64)
         nc.gpsimd.memset(scales[:], 0)
+        slot_words = [keep.tile([P, E * C], U32, name=f"slot_words{a}", align_bytes=64) for a in range(PASSES)]
+        slot_scales = keep.tile([P, E * C], U8, name="slot_scales", align_bytes=64)
         windows = [keep.tile([P, T], F32, name=f"window{b}", align_bytes=64) for b in range(OUT_TILES)]
-        slot_words0 = keep.tile([P, E * C], U32, name="slot_words0", align_bytes=64)
-        gate_sb, w1_words, w1_scales = {}, {}, {}
 
-        x_raw, w1_raw, w2_raw = {}, {}, {}
+        x_raw, w1_raw, w2_raw, gate_sb = {}, {}, {}, {}
 
         def load_x(a):
             rows = xT.rearrange("(a p j) n -> a p j n", p=P, j=PACK)[a]
-            first = 0
-            for width in X_LOADS[a]:
-                tag, bufs = ("raw", RAW_BUFS) if width <= CHUNK else (f"x_raw{a}", 1)
-                raw = raw_pool.tile([P, PACK, width], F32, name=tag, align_bytes=64, bufs=bufs)
-                nc.sync.dma_start(raw[:], rows[:, :, first : first + width])
-                for token in range(first, first + width, P):
-                    x_raw[a, token] = (raw, first)
-                first += width
+            long = keep.tile([P, PACK, LONG], F32, name=f"x_long{a}", align_bytes=64)
+            nc.sync.dma_start(long[:], rows[:, :, :LONG])
+            short = raw_pool.tile([P, PACK, T - LONG], F32, name="raw", align_bytes=64)
+            nc.sync.dma_start(short[:], rows[:, :, LONG:])
+            x_raw[a] = [long[:, :, :CHUNK], long[:, :, CHUNK:], short[:]]
 
         def load_w1(e, a):
             w1_raw[e, a] = raw_pool.tile([P, PACK, H], F32, name="raw", align_bytes=64)
@@ -101,9 +83,9 @@ def tile_routed_moe_kernel(tc, xT, w1, w2, gate, offs, out):
 
         def load_w2(e):
             w2_raw[e] = keep.tile([P, PACK, N], F32, name=f"w2_raw{e}", align_bytes=64)
-            rows = w2[e].rearrange("(r t s) n -> s r t n", t=PACK, s=2)
-            for s in range(2):
-                nc.sync.dma_start(w2_raw[e][s:P:2], rows[s])
+            rows = w2[e].rearrange("(r t s) n -> s r t n", t=PACK, s=PAIR)
+            for s in range(PAIR):
+                nc.sync.dma_start(w2_raw[e][s:P:PAIR], rows[s])
 
         def load_gate(e, b):
             gate_sb[e, b] = keep.tile([P, C], F32, name=f"gate_sb{e}_{b}", align_bytes=64)
@@ -112,90 +94,69 @@ def tile_routed_moe_kernel(tc, xT, w1, w2, gate, offs, out):
         load_x(0)
         nc.sync.dma_start(slots_list[:], offs)
         load_x(1)
-        pieces = E * PASSES
-        for step in range(2 * pieces):
-            if step < pieces:
-                load_w1(step // PASSES, step % PASSES)
+        for half in range(HALVES + GATE_LAG + OUT_TILES - 1):
+            if half < HALVES:
+                load_w1(*divmod(half, PASSES))
             for e in range(E):
-                if step == W2_STEP[e]:
+                if half == min(PASSES * e + 1 + W2_LAG, HALVES):
                     load_w2(e)
             for e in range(E):
                 for b in range(OUT_TILES):
-                    if step == GATE_STEP[b][e]:
+                    if half == PASSES * e + 1 + GATE_LAG + b:
                         load_gate(e, b)
 
         for b in range(OUT_TILES):
             nc.vector.memset(windows[b][:], 0.0)
 
         def quantise_x(a):
-            first = 0
-            for c, width in enumerate(X_STEPS[a]):
-                grouped = x_pool.tile([P, width, PACK], BF16, name="x_grouped", align_bytes=64)
-                tile, start = x_raw[a, first]
-                raw = tile[:, :, first - start : first - start + width]
-                vector = X_VECTOR[a][c]
-                if vector > 0:
-                    interleave(nc.vector.tensor_copy, grouped[:, :vector], raw[:, :, :vector])
-                if vector < width:
-                    interleave(nc.scalar.copy, grouped[:, vector:], raw[:, :, vector:])
-                tokens = slice(first, first + width)
-                first += width
+            for c, raw in enumerate(x_raw[a]):
+                grouped = x_pool.tile([P, CHUNK, PACK], BF16, name="x_grouped", align_bytes=64)
+                interleave(nc.vector.tensor_copy, grouped[:, : CHUNK // 2], raw[:, :, : CHUNK // 2])
+                interleave(nc.scalar.copy, grouped[:, CHUNK // 2 :], raw[:, :, CHUNK // 2 :])
+                tokens = slice(c * CHUNK, (c + 1) * CHUNK)
                 nc.vector.quantize_mx(
                     out=words[a][:, tokens].bitcast(FP8X4),
-                    scales=scales[4 * a : P, tokens],
+                    scales=scales[SCALE_ROWS * a : P, tokens],
                     in_=grouped[:].rearrange("p c j -> p (c j)"),
                 )
 
-        def places(first, last):
-            return slots_list[:, first // LIST_ROWS : last // LIST_ROWS]
-
-        def gather_pass1(first, last):
-            slot_words1 = slot_pool.tile([P, last - first], U32, name="slot_words1", align_bytes=64)
-            slot_scales = slot_pool.tile([P, last - first], U8, name="slot_scales", align_bytes=64)
-            nc.vector.tensor_copy(slot_words1[:], words[1][:].indirect(places(first, last)))
-            nc.vector.tensor_copy(slot_scales[:], scales[:].indirect(places(first, last)))
-            return slot_words1, slot_scales, first
-
-        def quantise_w1(e, a):
-            if a == 0:
-                w1_words[e] = keep.tile([P, PASSES, H], U32, name=f"w1_words{e}", align_bytes=64)
-                w1_scales[e] = keep.tile([P, PASSES, H], U8, name=f"w1_scales{e}", align_bytes=64)
-            vector = W1_VECTOR[PASSES * e + a]
-            raw = w1_raw[e, a][:]
-            grouped = w1_pool.tile([P, H, PACK], BF16, name="w1_grouped", align_bytes=64)
-            if vector > 0:
-                interleave_w1(nc.vector.tensor_copy, grouped[:], raw, 0, vector)
-            piece = (P - vector) // W1_PIECES
-            for i in range(W1_PIECES if vector < P else 0):
-                interleave_w1(nc.scalar.copy, grouped[:], raw, vector + i * piece, vector + (i + 1) * piece)
-            nc.vector.quantize_mx(
-                out=w1_words[e][:, a].bitcast(FP8X4),
-                scales=w1_scales[e][:, a],
-                in_=grouped[:].rearrange("p h j -> p (h j)"),
-            )
-
-        def spent(step):
-            return w1_raw[step // PASSES, step % PASSES][:].rearrange("p j h -> p (j h)")
+        def quantise_w1(e):
+            w1_words = keep.tile([P, PASSES, H], U32, name=f"w1_words{e}", align_bytes=64)
+            w1_scales = keep.tile([P, PASSES, H], U8, name=f"w1_scales{e}", align_bytes=64)
+            groups = P // PAIR
+            for a in range(PASSES):
+                grouped = w1_pool.tile([P, H, PACK], BF16, name="w1_grouped", align_bytes=64)
+                shared = e > 0 and (e, a) != (E - 1, PASSES - 1)
+                vector = groups // 2 if shared else 0
+                if shared:
+                    interleave_w1(nc.vector.tensor_copy, grouped[:], w1_raw[e, a][:], slice(0, vector))
+                interleave_w1(nc.scalar.copy, grouped[:], w1_raw[e, a][:], slice(vector, groups))
+                nc.vector.quantize_mx(
+                    out=w1_words[:, a].bitcast(FP8X4),
+                    scales=w1_scales[:, a],
+                    in_=grouped[:].rearrange("p h j -> p (h j)"),
+                )
+            return w1_words, w1_scales
 
         def quantise_w2(e):
             w2_words = keep.tile([P, N], U32, name=f"w2_words{e}", align_bytes=64)
             w2_scales = keep.tile([P, N], U8, name=f"w2_scales{e}", align_bytes=64)
             grouped = w2_pool.tile([P, N, PACK], BF16, name="w2_grouped", align_bytes=64)
-            vector = W2_VECTOR[e]
-            if vector > 0:
-                interleave(nc.vector.tensor_copy, grouped[:, :vector], w2_raw[e][:, :, :vector])
-            if vector < N:
-                interleave(nc.scalar.copy, grouped[:, vector:], w2_raw[e][:, :, vector:])
+            interleave(nc.vector.tensor_copy, grouped[:], w2_raw[e][:])
             nc.vector.quantize_mx(
                 out=w2_words[:].bitcast(FP8X4), scales=w2_scales[:], in_=grouped[:].rearrange("p n j -> p (n j)")
             )
             return w2_words, w2_scales
 
-        def layer1(e, slot_words1, slot_scales, first):
-            slots = slice(C * e - first, C * (e + 1) - first)
-            slot_words = (slot_words0[:, C * e : C * (e + 1)], slot_words1[:, slots])
+        def scratch(host, first, width, name):
+            if host < E:
+                return w1_raw[host, PASSES - 1][:].rearrange("p j h -> p (j h)")[:, first : first + width]
+            return keep.tile([P, width], F32, name=name, align_bytes=64)[:]
+
+        def layer1(e, w1_words, w1_scales):
+            slots = slice(C * e, C * (e + 1))
             banks = []
-            for u in range(TILES // BANK_TILES):
+            for u in range(BANKS):
                 sums = h_psum.tile([P, BANK_TILES, C], F32, name="h_sums")
                 banks.append(sums)
                 for i in range(BANK_TILES):
@@ -204,47 +165,36 @@ def tile_routed_moe_kernel(tc, xT, w1, w2, gate, offs, out):
                     for a in range(PASSES):
                         nc.tensor.matmul_mx(
                             out=sums[:, i],
-                            lhsT=w1_words[e][:, a, columns].bitcast(FP8X4),
-                            lhsT_scale=w1_scales[e][:, a, columns],
-                            rhs=slot_words[a].bitcast(FP8X4),
-                            rhs_scale=slot_scales[4 * a : P, slots],
+                            lhsT=w1_words[:, a, columns].bitcast(FP8X4),
+                            lhsT_scale=w1_scales[:, a, columns],
+                            rhs=slot_words[a][:, slots].bitcast(FP8X4),
+                            rhs_scale=slot_scales[SCALE_ROWS * a : P, slots],
                             start=(a == 0),
                             stop=(a == PASSES - 1),
                         )
             return banks
 
-        def rectify(e, step, banks):
-            if RELU_HOST and step < pieces and RELU_LAG[e] > 0:
-                flat = spent(step)[:, 2 * H :]
-            else:
-                flat = relu_pool.tile([P, TILES * C], F32, name="relu", align_bytes=64)[:]
-            relu = flat.rearrange("p (u n i) -> p u n i", u=TILES // BANK_TILES, i=BANK_TILES)
-            for u in range(TILES // BANK_TILES):
+        def rectify(e, banks):
+            flat = scratch(e + 1, TILES * C, TILES * C, f"relu{e}")
+            relu = flat.rearrange("p (u n i) -> p u n i", u=BANKS, i=BANK_TILES)
+            for u in range(BANKS):
                 nc.scalar.activation(relu[:, u], banks[u][:].rearrange("p i n -> p n i"), RELU)
             return relu
 
-        def square(e, step, relu):
-            if SQUARE_HOST and step < pieces and SQUARE_LAG[e] > 0:
-                flat = spent(step)[:, H : 2 * H].bitcast(BF16)
-            else:
-                flat = h_pool.tile([P, C * PACK], BF16, name="h_grouped", align_bytes=64)[:]
-            grouped = flat.rearrange("p (n u i) -> p n u i", u=TILES // BANK_TILES, i=BANK_TILES)
-            source = relu.rearrange("p u n i -> p n u i")
-            scalar_slots = C - SQ_VECTOR[e]
-            nc.scalar.activation(grouped[:, :scalar_slots], source[:, :scalar_slots], SQUARE)
-            if scalar_slots < C:
-                nc.vector.tensor_tensor(grouped[:, scalar_slots:], source[:, scalar_slots:], source[:, scalar_slots:], MULT)
+        def quantise_h(e, relu):
+            grouped = h_pool.tile([P, C, PACK], BF16, name="h_grouped", align_bytes=64)
+            nc.scalar.activation(
+                grouped[:].rearrange("p n (u i) -> p n u i", u=BANKS), relu.rearrange("p u n i -> p n u i"), SQUARE
+            )
             h_words = keep.tile([P, C], U32, name=f"h_words{e}", align_bytes=64)
             h_scales = keep.tile([P, C], U8, name=f"h_scales{e}", align_bytes=64)
-            nc.vector.quantize_mx(out=h_words[:].bitcast(FP8X4), scales=h_scales[:], in_=flat)
+            nc.vector.quantize_mx(
+                out=h_words[:].bitcast(FP8X4), scales=h_scales[:], in_=grouped[:].rearrange("p n j -> p (n j)")
+            )
             return h_words, h_scales
 
-        def layer2(e, step, w2_words, w2_scales, h_words, h_scales):
-            if Y_HOST and step < pieces and Y_LAG[e] > 0:
-                flat = spent(step)[:, :H]
-            else:
-                flat = keep.tile([P, OUT_TILES * C], F32, name=f"y{e}", align_bytes=64)[:]
-            y = flat.rearrange("p (b c) -> p b c", b=OUT_TILES)
+        def layer2(e, h_words, h_scales, w2_words, w2_scales):
+            y = scratch(e + 2, 0, OUT_TILES * C, f"y{e}").rearrange("p (b c) -> p b c", b=OUT_TILES)
             for b in range(OUT_TILES):
                 features = slice(P * b, P * (b + 1))
                 sums = y_psum.tile([P, C], F32, name="y_sums")
@@ -261,33 +211,24 @@ def tile_routed_moe_kernel(tc, xT, w1, w2, gate, offs, out):
             return y
 
         def scatter(e, y):
+            places = slots_list[:, C // LIST_ROWS * e : C // LIST_ROWS * (e + 1)]
             for b in range(OUT_TILES):
-                nc.vector.tensor_tensor(
-                    windows[b][:].indirect(places(C * e, C * (e + 1))), y[:, b], gate_sb[e, b][:], MULT
-                )
+                nc.vector.tensor_tensor(windows[b][:].indirect(places), y[:, b], gate_sb[e, b][:], MULT)
 
-        quantise_x(0)
-        quantise_x(1)
-        nc.vector.tensor_copy(slot_words0[:], words[0][:].indirect(slots_list[:]))
-        stage = {}
-        for step in range(2 * pieces):
-            if step < pieces:
-                e, a = divmod(step, PASSES)
-                if a == 0 and C * e in GCUTS:
-                    gathered = gather_pass1(C * e, GCUTS[GCUTS.index(C * e) + 1])
-                quantise_w1(e, a)
-                if a == PASSES - 1:
-                    stage[e] = layer1(e, *gathered)
-            for e in range(E):
-                age = step - (PASSES * e + 1)
-                if age == RELU_LAG[e]:
-                    stage[e] = rectify(e, step, stage[e])
-                if age == SQUARE_LAG[e]:
-                    stage[e] = square(e, step, stage[e])
-                if age == Y_LAG[e]:
-                    stage[e] = layer2(e, step, *quantise_w2(e), *stage[e])
-                if age == SCATTER_LAG[e]:
-                    scatter(e, stage[e])
+        for a in range(PASSES):
+            quantise_x(a)
+        for a in range(PASSES):
+            nc.vector.tensor_copy(slot_words[a][:], words[a][:].indirect(slots_list[:]))
+        nc.vector.tensor_copy(slot_scales[:], scales[:].indirect(slots_list[:]))
+
+        banks, relus = {}, {}
+        for r in range(E + 2):
+            if r < E:
+                banks[r] = layer1(r, *quantise_w1(r))
+            if r >= 2:
+                scatter(r - 2, layer2(r - 2, *quantise_h(r - 2, relus[r - 2]), *quantise_w2(r - 2)))
+            if 1 <= r <= E:
+                relus[r - 1] = rectify(r - 1, banks[r - 1])
 
         for b in range(OUT_TILES):
             nc.sync.dma_start(out[P * b : P * (b + 1), :], windows[b][:])

@@ -12,6 +12,7 @@ U16 = mybir.dt.uint16
 U8 = mybir.dt.uint8
 FP8X4 = mybir.dt.float8_e4m3fn_x4
 MULT = mybir.AluOpType.mult
+COPY = mybir.ActivationFunctionType.Copy
 RELU = mybir.ActivationFunctionType.Relu
 SQUARE = mybir.ActivationFunctionType.Square
 
@@ -28,9 +29,9 @@ LIST_ROWS = 16
 SCALE_ROWS = 4
 CHUNK = 512
 LONG = 2 * CHUNK
-
-W2_LAG = 2
-GATE_LAG = 4
+BUFFER = PACK * H * 4
+LAST = E - 1
+X_VECTOR = CHUNK // 2
 
 
 def interleave(copy, grouped, raw):
@@ -51,13 +52,14 @@ def tile_routed_moe_kernel(tc, xT, w1, w2, gate, offs, out):
     nc = tc.nc
     with ExitStack() as ctx:
         keep = ctx.enter_context(tc.tile_pool(name="keep", bufs=1))
-        raw_pool = ctx.enter_context(tc.tile_pool(name="raw_pool", bufs=8))
+        placed = ctx.enter_context(tc.tile_pool(name="placed", bufs=1))
         x_pool = ctx.enter_context(tc.tile_pool(name="x_pool", bufs=3))
-        w1_pool = ctx.enter_context(tc.tile_pool(name="w1_pool", bufs=3))
-        w2_pool = ctx.enter_context(tc.tile_pool(name="w2_pool", bufs=2))
         h_pool = ctx.enter_context(tc.tile_pool(name="h_pool", bufs=2))
         h_psum = ctx.enter_context(tc.psum_pool(name="h_psum", bufs=2 * BANKS))
         y_psum = ctx.enter_context(tc.psum_pool(name="y_psum", bufs=2 * OUT_TILES))
+
+        def place(shape, dtype, name, offset):
+            return placed.tile(shape, dtype, name=name, align_bytes=64, offset=offset)
 
         slots_list = keep.tile([P, E * C // LIST_ROWS], U16, name="slots_list", align_bytes=64)
         words = [keep.tile([P, T], U32, name=f"words{a}", align_bytes=64) for a in range(PASSES)]
@@ -73,12 +75,12 @@ def tile_routed_moe_kernel(tc, xT, w1, w2, gate, offs, out):
             rows = xT.rearrange("(a p j) n -> a p j n", p=P, j=PACK)[a]
             long = keep.tile([P, PACK, LONG], F32, name=f"x_long{a}", align_bytes=64)
             nc.sync.dma_start(long[:], rows[:, :, :LONG])
-            short = raw_pool.tile([P, PACK, T - LONG], F32, name="raw", align_bytes=64)
+            short = place([P, PACK, T - LONG], F32, f"x_short{a}", BUFFER * (HALVES - PASSES + a))
             nc.sync.dma_start(short[:], rows[:, :, LONG:])
             x_raw[a] = [long[:, :, :CHUNK], long[:, :, CHUNK:], short[:]]
 
         def load_w1(e, a):
-            w1_raw[e, a] = raw_pool.tile([P, PACK, H], F32, name="raw", align_bytes=64)
+            w1_raw[e, a] = place([P, PACK, H], F32, f"w1_raw{e}_{a}", BUFFER * (PASSES * e + a))
             nc.sync.dma_start(w1_raw[e, a][:], w1[e].rearrange("(a p j) h -> a p j h", p=P, j=PACK)[a])
 
         def load_w2(e):
@@ -87,23 +89,22 @@ def tile_routed_moe_kernel(tc, xT, w1, w2, gate, offs, out):
             for s in range(PAIR):
                 nc.sync.dma_start(w2_raw[e][s:P:PAIR], rows[s])
 
-        def load_gate(e, b):
-            gate_sb[e, b] = keep.tile([P, C], F32, name=f"gate_sb{e}_{b}", align_bytes=64)
-            nc.sync.dma_start(gate_sb[e, b][:], gate[P * b : P * (b + 1), C * e : C * (e + 1)])
+        def load_gate(e):
+            gate_sb[e] = keep.tile([P, OUT_TILES, C], F32, name=f"gate_sb{e}", align_bytes=64)
+            nc.sync.dma_start(gate_sb[e][:], gate.rearrange("(b p) j -> p b j", p=P)[:, :, C * e : C * (e + 1)])
 
         load_x(0)
         nc.sync.dma_start(slots_list[:], offs)
         load_x(1)
-        for half in range(HALVES + GATE_LAG + OUT_TILES - 1):
-            if half < HALVES:
-                load_w1(*divmod(half, PASSES))
-            for e in range(E):
-                if half == min(PASSES * e + 1 + W2_LAG, HALVES):
-                    load_w2(e)
-            for e in range(E):
-                for b in range(OUT_TILES):
-                    if half == PASSES * e + 1 + GATE_LAG + b:
-                        load_gate(e, b)
+        for half in range(HALVES):
+            load_w1(*divmod(half, PASSES))
+            if half >= 2 * PASSES and half % PASSES == 0:
+                load_gate(half // PASSES - 2)
+            if PASSES <= half < PASSES + LAST:
+                load_w2(half - PASSES)
+        load_gate(LAST - 1)
+        load_w2(LAST)
+        load_gate(LAST)
 
         for b in range(OUT_TILES):
             nc.vector.memset(windows[b][:], 0.0)
@@ -111,8 +112,8 @@ def tile_routed_moe_kernel(tc, xT, w1, w2, gate, offs, out):
         def quantise_x(a):
             for c, raw in enumerate(x_raw[a]):
                 grouped = x_pool.tile([P, CHUNK, PACK], BF16, name="x_grouped", align_bytes=64)
-                interleave(nc.vector.tensor_copy, grouped[:, : CHUNK // 2], raw[:, :, : CHUNK // 2])
-                interleave(nc.scalar.copy, grouped[:, CHUNK // 2 :], raw[:, :, CHUNK // 2 :])
+                interleave(nc.vector.tensor_copy, grouped[:, :X_VECTOR], raw[:, :, :X_VECTOR])
+                interleave(nc.scalar.copy, grouped[:, X_VECTOR:], raw[:, :, X_VECTOR:])
                 tokens = slice(c * CHUNK, (c + 1) * CHUNK)
                 nc.vector.quantize_mx(
                     out=words[a][:, tokens].bitcast(FP8X4),
@@ -120,86 +121,87 @@ def tile_routed_moe_kernel(tc, xT, w1, w2, gate, offs, out):
                     in_=grouped[:].rearrange("p c j -> p (c j)"),
                 )
 
-        def quantise_w1(e):
-            w1_words = keep.tile([P, PASSES, H], U32, name=f"w1_words{e}", align_bytes=64)
-            w1_scales = keep.tile([P, PASSES, H], U8, name=f"w1_scales{e}", align_bytes=64)
+        def round_w1(e, a):
+            grouped = x_pool.tile([P, H, PACK], BF16, name="w1_grouped", align_bytes=64)
             groups = P // PAIR
-            for a in range(PASSES):
-                grouped = w1_pool.tile([P, H, PACK], BF16, name="w1_grouped", align_bytes=64)
-                shared = e > 0 and (e, a) != (E - 1, PASSES - 1)
-                vector = groups // 2 if shared else 0
-                if shared:
-                    interleave_w1(nc.vector.tensor_copy, grouped[:], w1_raw[e, a][:], slice(0, vector))
-                interleave_w1(nc.scalar.copy, grouped[:], w1_raw[e, a][:], slice(vector, groups))
-                nc.vector.quantize_mx(
-                    out=w1_words[:, a].bitcast(FP8X4),
-                    scales=w1_scales[:, a],
-                    in_=grouped[:].rearrange("p h j -> p (h j)"),
-                )
-            return w1_words, w1_scales
+            scalar = groups if e == 0 else groups // 2 if (e, a) == (1, 0) else 0
+            if scalar > 0:
+                interleave_w1(nc.scalar.copy, grouped[:], w1_raw[e, a][:], slice(0, scalar))
+            if scalar < groups:
+                interleave_w1(nc.vector.tensor_copy, grouped[:], w1_raw[e, a][:], slice(scalar, groups))
+            return grouped
 
         def quantise_w2(e):
-            w2_words = keep.tile([P, N], U32, name=f"w2_words{e}", align_bytes=64)
+            host = min(PASSES * (e + 1), HALVES - 1)
+            w2_words = place([P, N], U32, f"w2_words{e}", BUFFER * host + BUFFER // 4)
             w2_scales = keep.tile([P, N], U8, name=f"w2_scales{e}", align_bytes=64)
-            grouped = w2_pool.tile([P, N, PACK], BF16, name="w2_grouped", align_bytes=64)
-            interleave(nc.vector.tensor_copy, grouped[:], w2_raw[e][:])
+            if e < LAST:
+                grouped = h_pool.tile([P, N, PACK], BF16, name="w2_grouped", align_bytes=64)
+            else:
+                grouped = place([P, N, PACK], BF16, "w2_grouped_last", BUFFER * host + BUFFER // 2)
+            interleave(nc.scalar.copy if e < LAST else nc.vector.tensor_copy, grouped[:], w2_raw[e][:])
             nc.vector.quantize_mx(
                 out=w2_words[:].bitcast(FP8X4), scales=w2_scales[:], in_=grouped[:].rearrange("p n j -> p (n j)")
             )
             return w2_words, w2_scales
 
-        def scratch(host, first, width, name):
-            if host < E:
-                return w1_raw[host, PASSES - 1][:].rearrange("p j h -> p (j h)")[:, first : first + width]
-            return keep.tile([P, width], F32, name=name, align_bytes=64)[:]
+        h_sums = {}
 
-        def layer1(e, w1_words, w1_scales):
+        def layer1(e, a, grouped):
+            w1_words = keep.tile([P, H], U32, name=f"w1_words{e}_{a}", align_bytes=64)
+            w1_scales = keep.tile([P, H], U8, name=f"w1_scales{e}_{a}", align_bytes=64)
+            nc.vector.quantize_mx(
+                out=w1_words[:].bitcast(FP8X4), scales=w1_scales[:], in_=grouped[:].rearrange("p h j -> p (h j)")
+            )
             slots = slice(C * e, C * (e + 1))
-            banks = []
             for u in range(BANKS):
-                sums = h_psum.tile([P, BANK_TILES, C], F32, name="h_sums")
-                banks.append(sums)
+                if a == 0:
+                    h_sums[e, u] = h_psum.tile([P, BANK_TILES, C], F32, name="h_sums")
                 for i in range(BANK_TILES):
                     t = BANK_TILES * u + i
                     columns = slice(P * t, P * (t + 1))
-                    for a in range(PASSES):
-                        nc.tensor.matmul_mx(
-                            out=sums[:, i],
-                            lhsT=w1_words[:, a, columns].bitcast(FP8X4),
-                            lhsT_scale=w1_scales[:, a, columns],
-                            rhs=slot_words[a][:, slots].bitcast(FP8X4),
-                            rhs_scale=slot_scales[SCALE_ROWS * a : P, slots],
-                            start=(a == 0),
-                            stop=(a == PASSES - 1),
-                        )
-            return banks
+                    nc.tensor.matmul_mx(
+                        out=h_sums[e, u][:, i],
+                        lhsT=w1_words[:, columns].bitcast(FP8X4),
+                        lhsT_scale=w1_scales[:, columns],
+                        rhs=slot_words[a][:, slots].bitcast(FP8X4),
+                        rhs_scale=slot_scales[SCALE_ROWS * a : P, slots],
+                        start=(a == 0 and i == 0),
+                        stop=(a == PASSES - 1 and i == BANK_TILES - 1),
+                    )
 
-        def rectify(e, banks):
-            flat = scratch(e + 1, TILES * C, TILES * C, f"relu{e}")
-            relu = flat.rearrange("p (u n i) -> p u n i", u=BANKS, i=BANK_TILES)
+        relus = {}
+
+        def activate(e):
+            if e == 0:
+                relus[e] = w2_raw[e][:].rearrange("p j n -> p (j n)")
+            else:
+                relus[e] = h_pool.tile([P, TILES * C], F32, name="relu", align_bytes=64)[:]
+            relu = relus[e].rearrange("p (u n i) -> p u n i", u=BANKS, i=BANK_TILES)
             for u in range(BANKS):
-                nc.scalar.activation(relu[:, u], banks[u][:].rearrange("p i n -> p n i"), RELU)
-            return relu
-
-        def quantise_h(e, relu):
+                nc.scalar.activation(relu[:, u], h_sums[e, u][:].rearrange("p i n -> p n i"), RELU)
             grouped = h_pool.tile([P, C, PACK], BF16, name="h_grouped", align_bytes=64)
             nc.scalar.activation(
                 grouped[:].rearrange("p n (u i) -> p n u i", u=BANKS), relu.rearrange("p u n i -> p n u i"), SQUARE
             )
-            h_words = keep.tile([P, C], U32, name=f"h_words{e}", align_bytes=64)
+            return grouped
+
+        y_sums = {}
+
+        def layer2(e, grouped, w2_words, w2_scales):
+            if e < LAST:
+                h_words = place([P, C], U32, f"h_words{e}", BUFFER * (PASSES * (e + 1) + 1))
+            else:
+                h_words = keep.tile([P, C], U32, name=f"h_words{e}", align_bytes=64)
             h_scales = keep.tile([P, C], U8, name=f"h_scales{e}", align_bytes=64)
             nc.vector.quantize_mx(
                 out=h_words[:].bitcast(FP8X4), scales=h_scales[:], in_=grouped[:].rearrange("p n j -> p (n j)")
             )
-            return h_words, h_scales
-
-        def layer2(e, h_words, h_scales, w2_words, w2_scales):
-            y = scratch(e + 2, 0, OUT_TILES * C, f"y{e}").rearrange("p (b c) -> p b c", b=OUT_TILES)
             for b in range(OUT_TILES):
                 features = slice(P * b, P * (b + 1))
-                sums = y_psum.tile([P, C], F32, name="y_sums")
+                y_sums[e, b] = y_psum.tile([P, C], F32, name="y_sums")
                 nc.tensor.matmul_mx(
-                    out=sums[:],
+                    out=y_sums[e, b][:],
                     lhsT=w2_words[:, features].bitcast(FP8X4),
                     lhsT_scale=w2_scales[:, features],
                     rhs=h_words[:].bitcast(FP8X4),
@@ -207,28 +209,50 @@ def tile_routed_moe_kernel(tc, xT, w1, w2, gate, offs, out):
                     start=True,
                     stop=True,
                 )
-                nc.scalar.copy(y[:, b], sums[:])
-            return y
 
-        def scatter(e, y):
-            places = slots_list[:, C // LIST_ROWS * e : C // LIST_ROWS * (e + 1)]
-            for b in range(OUT_TILES):
-                nc.vector.tensor_tensor(windows[b][:].indirect(places), y[:, b], gate_sb[e, b][:], MULT)
+        def window(e, b):
+            return windows[b][:].indirect(slots_list[:, C // LIST_ROWS * e : C // LIST_ROWS * (e + 1)])
+
+        def scalar_scatter(e, b, gated):
+            nc.vector.tensor_tensor(gated, y_sums[e, b][:], gate_sb[e][:, b], MULT)
+            nc.scalar.activation(window(e, b), gated, COPY)
+
+        def vector_scatter(e, b, gated):
+            nc.vector.tensor_tensor(gated, y_sums[e, b][:], gate_sb[e][:, b], MULT)
+            nc.vector.tensor_copy(window(e, b), gated)
 
         for a in range(PASSES):
             quantise_x(a)
-        for a in range(PASSES):
             nc.vector.tensor_copy(slot_words[a][:], words[a][:].indirect(slots_list[:]))
         nc.vector.tensor_copy(slot_scales[:], scales[:].indirect(slots_list[:]))
 
-        banks, relus = {}, {}
-        for r in range(E + 2):
-            if r < E:
-                banks[r] = layer1(r, *quantise_w1(r))
-            if r >= 2:
-                scatter(r - 2, layer2(r - 2, *quantise_h(r - 2, relus[r - 2]), *quantise_w2(r - 2)))
-            if 1 <= r <= E:
-                relus[r - 1] = rectify(r - 1, banks[r - 1])
+        for a in range(PASSES):
+            layer1(0, a, round_w1(0, a))
+        for e in range(E):
+            if e > 0:
+                h_grouped = activate(e)
+            if e < LAST:
+                grouped = round_w1(e + 1, 0)
+                if e > 0:
+                    gated = place([P, OUT_TILES, C], F32, f"gated{e - 1}", BUFFER * PASSES * (e + 1))
+                    for b in range(OUT_TILES):
+                        scalar_scatter(e - 1, b, gated[:, b])
+                layer1(e + 1, 0, grouped)
+            w2_codes = quantise_w2(e)
+            if e == 0:
+                h_grouped = activate(e)
+            if e < LAST:
+                grouped = round_w1(e + 1, 1)
+                layer2(e, h_grouped, *w2_codes)
+                layer1(e + 1, 1, grouped)
+            else:
+                gated = place([P, C], F32, "gated_late", BUFFER * (HALVES - 1) + BUFFER // 2)
+                vector_scatter(e - 1, 0, gated[:])
+                scalar_scatter(e - 1, 1, relus[e][:, :C])
+                layer2(e, h_grouped, *w2_codes)
+        gated = keep.tile([P, OUT_TILES, C], F32, name="gated", align_bytes=64)
+        scalar_scatter(LAST, 0, gated[:, 0])
+        vector_scatter(LAST, 1, gated[:, 1])
 
         for b in range(OUT_TILES):
             nc.sync.dma_start(out[P * b : P * (b + 1), :], windows[b][:])

@@ -22,8 +22,8 @@ PAIR = 2
 PASSES = K // (P * PACK)
 HALVES = E * PASSES
 TILES = H // P
-BANK_TILES = 2
-BANKS = TILES // BANK_TILES
+BANK_SLOTS = 128
+BANKS = C // BANK_SLOTS
 OUT_TILES = N // P
 LIST_ROWS = 16
 SCALE_ROWS = 4
@@ -89,22 +89,21 @@ def tile_routed_moe_kernel(tc, xT, w1, w2, gate, offs, out):
             for s in range(PAIR):
                 nc.sync.dma_start(w2_raw[e][s:P:PAIR], rows[s])
 
-        def load_gate(e):
-            gate_sb[e] = keep.tile([P, OUT_TILES, C], F32, name=f"gate_sb{e}", align_bytes=64)
-            nc.sync.dma_start(gate_sb[e][:], gate.rearrange("(b p) j -> p b j", p=P)[:, :, C * e : C * (e + 1)])
+        def load_gate(e, b):
+            gate_sb[e, b] = keep.tile([P, C], F32, name=f"gate_sb{e}_{b}", align_bytes=64)
+            nc.sync.dma_start(gate_sb[e, b][:], gate[P * b : P * (b + 1), C * e : C * (e + 1)])
 
         load_x(0)
         nc.sync.dma_start(slots_list[:], offs)
         load_x(1)
-        for half in range(HALVES):
-            load_w1(*divmod(half, PASSES))
-            if half >= 2 * PASSES and half % PASSES == 0:
-                load_gate(half // PASSES - 2)
-            if PASSES <= half < PASSES + LAST:
-                load_w2(half - PASSES)
-        load_gate(LAST - 1)
-        load_w2(LAST)
-        load_gate(LAST)
+        for e in range(E + 2):
+            for a in range(PASSES):
+                if e < E:
+                    load_w1(e, a)
+                if e >= 2:
+                    load_gate(e - 2, a)
+                if 1 <= e <= E and a == (0 if e < E else PASSES - 1):
+                    load_w2(e - 1)
 
         for b in range(OUT_TILES):
             nc.vector.memset(windows[b][:], 0.0)
@@ -124,79 +123,74 @@ def tile_routed_moe_kernel(tc, xT, w1, w2, gate, offs, out):
         def round_w1(e, a):
             grouped = x_pool.tile([P, H, PACK], BF16, name="w1_grouped", align_bytes=64)
             groups = P // PAIR
-            scalar = groups if e == 0 else groups // 2 if (e, a) == (1, 0) else 0
+            scalar = groups if e == 0 else groups // 2 if e < LAST and a == 0 else 0
             if scalar > 0:
                 interleave_w1(nc.scalar.copy, grouped[:], w1_raw[e, a][:], slice(0, scalar))
             if scalar < groups:
                 interleave_w1(nc.vector.tensor_copy, grouped[:], w1_raw[e, a][:], slice(scalar, groups))
             return grouped
 
-        def quantise_w2(e):
-            host = min(PASSES * (e + 1), HALVES - 1)
-            w2_words = place([P, N], U32, f"w2_words{e}", BUFFER * host + BUFFER // 4)
-            w2_scales = keep.tile([P, N], U8, name=f"w2_scales{e}", align_bytes=64)
-            if e < LAST:
-                grouped = h_pool.tile([P, N, PACK], BF16, name="w2_grouped", align_bytes=64)
+        def round_w2(e):
+            grouped = h_pool.tile([P, N, PACK], BF16, name="w2_grouped", align_bytes=64)
+            interleave(nc.scalar.copy if e == 0 else nc.vector.tensor_copy, grouped[:], w2_raw[e][:])
+            return grouped
+
+        def quantise(name, grouped, offset=None):
+            width = grouped.shape[1]
+            if offset is None:
+                codes = keep.tile([P, width], U32, name=f"{name}_words", align_bytes=64)
             else:
-                grouped = place([P, N, PACK], BF16, "w2_grouped_last", BUFFER * host + BUFFER // 2)
-            interleave(nc.scalar.copy if e < LAST else nc.vector.tensor_copy, grouped[:], w2_raw[e][:])
+                codes = place([P, width], U32, f"{name}_words", offset)
+            exponents = keep.tile([P, width], U8, name=f"{name}_scales", align_bytes=64)
             nc.vector.quantize_mx(
-                out=w2_words[:].bitcast(FP8X4), scales=w2_scales[:], in_=grouped[:].rearrange("p n j -> p (n j)")
+                out=codes[:].bitcast(FP8X4), scales=exponents[:], in_=grouped[:].rearrange("p c j -> p (c j)")
             )
-            return w2_words, w2_scales
+            return codes, exponents
 
         h_sums = {}
 
         def layer1(e, a, grouped):
-            w1_words = keep.tile([P, H], U32, name=f"w1_words{e}_{a}", align_bytes=64)
-            w1_scales = keep.tile([P, H], U8, name=f"w1_scales{e}_{a}", align_bytes=64)
-            nc.vector.quantize_mx(
-                out=w1_words[:].bitcast(FP8X4), scales=w1_scales[:], in_=grouped[:].rearrange("p h j -> p (h j)")
-            )
-            slots = slice(C * e, C * (e + 1))
+            w1_words, w1_scales = quantise(f"w1_{e}_{a}", grouped)
             for u in range(BANKS):
                 if a == 0:
-                    h_sums[e, u] = h_psum.tile([P, BANK_TILES, C], F32, name="h_sums")
-                for i in range(BANK_TILES):
-                    t = BANK_TILES * u + i
+                    h_sums[e, u] = h_psum.tile([P, TILES, BANK_SLOTS], F32, name="h_sums")
+                slots = slice(C * e + BANK_SLOTS * u, C * e + BANK_SLOTS * (u + 1))
+                for t in range(TILES):
                     columns = slice(P * t, P * (t + 1))
                     nc.tensor.matmul_mx(
-                        out=h_sums[e, u][:, i],
+                        out=h_sums[e, u][:, t],
                         lhsT=w1_words[:, columns].bitcast(FP8X4),
                         lhsT_scale=w1_scales[:, columns],
                         rhs=slot_words[a][:, slots].bitcast(FP8X4),
                         rhs_scale=slot_scales[SCALE_ROWS * a : P, slots],
-                        start=(a == 0 and i == 0),
-                        stop=(a == PASSES - 1 and i == BANK_TILES - 1),
+                        start=(a == 0 and t == 0),
+                        stop=(a == PASSES - 1 and t == TILES - 1),
                     )
 
-        relus = {}
-
-        def activate(e):
-            if e == 0:
-                relus[e] = w2_raw[e][:].rearrange("p j n -> p (j n)")
-            else:
-                relus[e] = h_pool.tile([P, TILES * C], F32, name="relu", align_bytes=64)[:]
-            relu = relus[e].rearrange("p (u n i) -> p u n i", u=BANKS, i=BANK_TILES)
-            for u in range(BANKS):
-                nc.scalar.activation(relu[:, u], h_sums[e, u][:].rearrange("p i n -> p n i"), RELU)
+        def activate(e, flat):
+            relu = flat.rearrange("p (u n t) -> p u n t", u=BANKS, t=TILES)
             grouped = h_pool.tile([P, C, PACK], BF16, name="h_grouped", align_bytes=64)
-            nc.scalar.activation(
-                grouped[:].rearrange("p n (u i) -> p n u i", u=BANKS), relu.rearrange("p u n i -> p n u i"), SQUARE
-            )
+            halves = grouped[:].rearrange("p (u n) t -> p u n t", u=BANKS)
+            on_scalar = range(BANKS if e < LAST else 1)
+            for u in range(BANKS):
+                sums = h_sums[e, u][:].rearrange("p t n -> p n t")
+                if u in on_scalar:
+                    nc.scalar.activation(relu[:, u], sums, RELU)
+                else:
+                    nc.vector.tensor_scalar_max(relu[:, u], sums, 0.0)
+            for u in range(BANKS):
+                if u in on_scalar:
+                    nc.scalar.activation(halves[:, u], relu[:, u], SQUARE)
+                else:
+                    nc.vector.tensor_tensor(halves[:, u], relu[:, u], relu[:, u], MULT)
             return grouped
 
         y_sums = {}
 
-        def layer2(e, grouped, w2_words, w2_scales):
-            if e < LAST:
-                h_words = place([P, C], U32, f"h_words{e}", BUFFER * (PASSES * (e + 1) + 1))
-            else:
-                h_words = keep.tile([P, C], U32, name=f"h_words{e}", align_bytes=64)
-            h_scales = keep.tile([P, C], U8, name=f"h_scales{e}", align_bytes=64)
-            nc.vector.quantize_mx(
-                out=h_words[:].bitcast(FP8X4), scales=h_scales[:], in_=grouped[:].rearrange("p n j -> p (n j)")
-            )
+        def layer2(e, h_grouped, w2_grouped):
+            held = BUFFER * (PASSES * (e + 1) + 1)
+            w2_words, w2_scales = quantise(f"w2_{e}", w2_grouped, held if e < LAST else None)
+            h_words, h_scales = quantise(f"h_{e}", h_grouped, held + 4 * N if e < LAST else None)
             for b in range(OUT_TILES):
                 features = slice(P * b, P * (b + 1))
                 y_sums[e, b] = y_psum.tile([P, C], F32, name="y_sums")
@@ -210,49 +204,54 @@ def tile_routed_moe_kernel(tc, xT, w1, w2, gate, offs, out):
                     stop=True,
                 )
 
-        def window(e, b):
-            return windows[b][:].indirect(slots_list[:, C // LIST_ROWS * e : C // LIST_ROWS * (e + 1)])
+        def apply_gate(e, b):
+            gated = keep.tile([P, C], F32, name=f"gated{e}_{b}", align_bytes=64)
+            nc.vector.tensor_tensor(gated[:], y_sums[e, b][:], gate_sb[e, b][:], MULT)
+            return gated
 
-        def scalar_scatter(e, b, gated):
-            nc.vector.tensor_tensor(gated, y_sums[e, b][:], gate_sb[e][:, b], MULT)
-            nc.scalar.activation(window(e, b), gated, COPY)
-
-        def vector_scatter(e, b, gated):
-            nc.vector.tensor_tensor(gated, y_sums[e, b][:], gate_sb[e][:, b], MULT)
-            nc.vector.tensor_copy(window(e, b), gated)
+        def scatter(e, b, gated):
+            window = windows[b][:].indirect(slots_list[:, C // LIST_ROWS * e : C // LIST_ROWS * (e + 1)])
+            if (e, b) == (LAST, 0):
+                nc.vector.tensor_copy(window, gated[:])
+            else:
+                nc.scalar.activation(window, gated[:], COPY)
 
         for a in range(PASSES):
             quantise_x(a)
             nc.vector.tensor_copy(slot_words[a][:], words[a][:].indirect(slots_list[:]))
         nc.vector.tensor_copy(slot_scales[:], scales[:].indirect(slots_list[:]))
 
+        def spent(raw):
+            return raw[:].rearrange("p j c -> p (j c)")[:, : TILES * C]
+
         for a in range(PASSES):
             layer1(0, a, round_w1(0, a))
-        for e in range(E):
-            if e > 0:
-                h_grouped = activate(e)
-            if e < LAST:
-                grouped = round_w1(e + 1, 0)
-                if e > 0:
-                    gated = place([P, OUT_TILES, C], F32, f"gated{e - 1}", BUFFER * PASSES * (e + 1))
-                    for b in range(OUT_TILES):
-                        scalar_scatter(e - 1, b, gated[:, b])
-                layer1(e + 1, 0, grouped)
-            w2_codes = quantise_w2(e)
-            if e == 0:
-                h_grouped = activate(e)
-            if e < LAST:
-                grouped = round_w1(e + 1, 1)
-                layer2(e, h_grouped, *w2_codes)
-                layer1(e + 1, 1, grouped)
-            else:
-                gated = place([P, C], F32, "gated_late", BUFFER * (HALVES - 1) + BUFFER // 2)
-                vector_scatter(e - 1, 0, gated[:])
-                scalar_scatter(e - 1, 1, relus[e][:, :C])
-                layer2(e, h_grouped, *w2_codes)
-        gated = keep.tile([P, OUT_TILES, C], F32, name="gated", align_bytes=64)
-        scalar_scatter(LAST, 0, gated[:, 0])
-        vector_scatter(LAST, 1, gated[:, 1])
+        layer1(1, 0, round_w1(1, 0))
+        w2_grouped = round_w2(0)
+        h_grouped = activate(0, spent(w2_raw[0]))
+        layer1(1, 1, round_w1(1, 1))
+        layer2(0, h_grouped, w2_grouped)
+        for e in range(1, LAST):
+            grouped = round_w1(e + 1, 0)
+            relu = spent(w1_raw[e + 1, 0]) if e == 1 else h_pool.tile([P, TILES * C], F32, name="relu")[:]
+            h_grouped = activate(e, relu)
+            scatter(e - 1, 0, apply_gate(e - 1, 0))
+            layer1(e + 1, 0, grouped)
+            w2_grouped = round_w2(e)
+            grouped = round_w1(e + 1, 1)
+            scatter(e - 1, 1, apply_gate(e - 1, 1))
+            if e + 1 < LAST:
+                layer2(e, h_grouped, w2_grouped)
+            layer1(e + 1, 1, grouped)
+        layer2(LAST - 1, h_grouped, w2_grouped)
+        w2_grouped = round_w2(LAST)
+        h_grouped = activate(LAST, h_pool.tile([P, TILES * C], F32, name="relu")[:])
+        for e in (LAST - 1, LAST):
+            if e == LAST:
+                layer2(e, h_grouped, w2_grouped)
+            gated = [apply_gate(e, b) for b in range(OUT_TILES)]
+            for b in range(OUT_TILES):
+                scatter(e, b, gated[b])
 
         for b in range(OUT_TILES):
             nc.sync.dma_start(out[P * b : P * (b + 1), :], windows[b][:])

@@ -102,7 +102,7 @@ def tile_routed_moe_kernel(tc, xT, w1, w2, gate, offs, out):
                     load_w1(e, a)
                 if e >= 2:
                     load_gate(e - 2, a)
-                if 1 <= e <= E and a == (0 if e < E else PASSES - 1):
+                if 1 <= e <= E and a == (0 if e in (1, E) else 1):
                     load_w2(e - 1)
 
         for b in range(OUT_TILES):
@@ -123,7 +123,7 @@ def tile_routed_moe_kernel(tc, xT, w1, w2, gate, offs, out):
         def round_w1(e, a):
             grouped = x_pool.tile([P, H, PACK], BF16, name="w1_grouped", align_bytes=64)
             groups = P // PAIR
-            scalar = groups if e == 0 else groups // 2 if e < LAST and a == 0 else 0
+            scalar = groups if e == 0 else groups // 2 if (e, a) == (1, 0) else 0
             if scalar > 0:
                 interleave_w1(nc.scalar.copy, grouped[:], w1_raw[e, a][:], slice(0, scalar))
             if scalar < groups:
@@ -171,7 +171,7 @@ def tile_routed_moe_kernel(tc, xT, w1, w2, gate, offs, out):
             relu = flat.rearrange("p (u n t) -> p u n t", u=BANKS, t=TILES)
             grouped = h_pool.tile([P, C, PACK], BF16, name="h_grouped", align_bytes=64)
             halves = grouped[:].rearrange("p (u n) t -> p u n t", u=BANKS)
-            on_scalar = range(BANKS if e < LAST else 1)
+            on_scalar = range(0 if e < LAST else 1, BANKS)
             for u in range(BANKS):
                 sums = h_sums[e, u][:].rearrange("p t n -> p n t")
                 if u in on_scalar:
@@ -189,8 +189,11 @@ def tile_routed_moe_kernel(tc, xT, w1, w2, gate, offs, out):
 
         def layer2(e, h_grouped, w2_grouped):
             held = BUFFER * (PASSES * (e + 1) + 1)
-            w2_words, w2_scales = quantise(f"w2_{e}", w2_grouped, held if e < LAST else None)
-            h_words, h_scales = quantise(f"h_{e}", h_grouped, held + 4 * N if e < LAST else None)
+            if e < LAST:
+                h_words, h_scales = quantise(f"h_{e}", h_grouped, held)
+            w2_words, w2_scales = quantise(f"w2_{e}", w2_grouped, held + 4 * C if e == 0 else None)
+            if e == LAST:
+                h_words, h_scales = quantise(f"h_{e}", h_grouped)
             for b in range(OUT_TILES):
                 features = slice(P * b, P * (b + 1))
                 y_sums[e, b] = y_psum.tile([P, C], F32, name="y_sums")
@@ -232,26 +235,20 @@ def tile_routed_moe_kernel(tc, xT, w1, w2, gate, offs, out):
         layer1(1, 1, round_w1(1, 1))
         layer2(0, h_grouped, w2_grouped)
         for e in range(1, LAST):
-            grouped = round_w1(e + 1, 0)
-            relu = spent(w1_raw[e + 1, 0]) if e == 1 else h_pool.tile([P, TILES * C], F32, name="relu")[:]
-            h_grouped = activate(e, relu)
-            scatter(e - 1, 0, apply_gate(e - 1, 0))
-            layer1(e + 1, 0, grouped)
-            w2_grouped = round_w2(e)
-            grouped = round_w1(e + 1, 1)
-            scatter(e - 1, 1, apply_gate(e - 1, 1))
-            if e + 1 < LAST:
-                layer2(e, h_grouped, w2_grouped)
-            layer1(e + 1, 1, grouped)
-        layer2(LAST - 1, h_grouped, w2_grouped)
+            h_grouped = activate(e, h_pool.tile([P, TILES * C], F32, name="relu")[:])
+            for a in range(PASSES):
+                grouped = round_w1(e + 1, a)
+                scatter(e - 1, a, apply_gate(e - 1, a))
+                layer1(e + 1, a, grouped)
+            layer2(e, h_grouped, round_w2(e))
         w2_grouped = round_w2(LAST)
         h_grouped = activate(LAST, h_pool.tile([P, TILES * C], F32, name="relu")[:])
-        for e in (LAST - 1, LAST):
-            if e == LAST:
-                layer2(e, h_grouped, w2_grouped)
-            gated = [apply_gate(e, b) for b in range(OUT_TILES)]
-            for b in range(OUT_TILES):
-                scatter(e, b, gated[b])
+        scatter(LAST - 1, 0, apply_gate(LAST - 1, 0))
+        layer2(LAST, h_grouped, w2_grouped)
+        scatter(LAST - 1, 1, apply_gate(LAST - 1, 1))
+        gated = [apply_gate(LAST, b) for b in range(OUT_TILES)]
+        for b in range(OUT_TILES):
+            scatter(LAST, b, gated[b])
 
         for b in range(OUT_TILES):
             nc.sync.dma_start(out[P * b : P * (b + 1), :], windows[b][:])

@@ -43,8 +43,8 @@ def interleave(copy, grouped, raw):
 
 def interleave_w1(copy, grouped, raw, groups):
     copy(
-        grouped.rearrange("p (t r s) j -> p r t j s", t=TILES, s=PAIR)[:, groups],
-        raw.rearrange("p j (r t s) -> p r t j s", t=TILES, s=PAIR)[:, groups],
+        grouped.rearrange("p (u v m) j -> p u m j v", u=TILES // PAIR, v=PAIR)[:, :, groups],
+        raw.rearrange("p j (m u v) -> p u m j v", u=TILES // PAIR, v=PAIR)[:, :, groups],
     )
 
 
@@ -85,9 +85,7 @@ def tile_routed_moe_kernel(tc, xT, w1, w2, gate, offs, out):
 
         def load_w2(e):
             w2_raw[e] = keep.tile([P, PACK, N], F32, name=f"w2_raw{e}", align_bytes=64)
-            rows = w2[e].rearrange("(r t s) n -> s r t n", t=PACK, s=PAIR)
-            for s in range(PAIR):
-                nc.sync.dma_start(w2_raw[e][s:P:PAIR], rows[s])
+            nc.sync.dma_start(w2_raw[e][:], w2[e].rearrange("(p t) n -> p t n", t=PACK))
 
         def load_gate(e, b):
             gate_sb[e, b] = keep.tile([P, C], F32, name=f"gate_sb{e}_{b}", align_bytes=64)
@@ -122,7 +120,7 @@ def tile_routed_moe_kernel(tc, xT, w1, w2, gate, offs, out):
 
         def round_w1(e, a):
             grouped = x_pool.tile([P, H, PACK], BF16, name="w1_grouped", align_bytes=64)
-            groups = P // PAIR
+            groups = P
             scalar = groups if e == 0 else groups // 2 if (e, a) == (1, 0) else 0
             if scalar > 0:
                 interleave_w1(nc.scalar.copy, grouped[:], w1_raw[e, a][:], slice(0, scalar))

@@ -31,7 +31,7 @@ CHUNK = 512
 LONG = 2 * CHUNK
 BUFFER = PACK * H * 4
 LAST = E - 1
-X_VECTOR = CHUNK // 2
+X_VECTOR = (9 * CHUNK // 16, 9 * CHUNK // 16, CHUNK // 2)
 
 
 def interleave(copy, grouped, raw):
@@ -109,8 +109,9 @@ def tile_routed_moe_kernel(tc, xT, w1, w2, gate, offs, out):
         def quantise_x(a):
             for c, raw in enumerate(x_raw[a]):
                 grouped = x_pool.tile([P, CHUNK, PACK], BF16, name="x_grouped", align_bytes=64)
-                interleave(nc.vector.tensor_copy, grouped[:, :X_VECTOR], raw[:, :, :X_VECTOR])
-                interleave(nc.scalar.copy, grouped[:, X_VECTOR:], raw[:, :, X_VECTOR:])
+                share = X_VECTOR[c]
+                interleave(nc.vector.tensor_copy, grouped[:, :share], raw[:, :, :share])
+                interleave(nc.scalar.copy, grouped[:, share:], raw[:, :, share:])
                 tokens = slice(c * CHUNK, (c + 1) * CHUNK)
                 nc.vector.quantize_mx(
                     out=words[a][:, tokens].bitcast(FP8X4),
@@ -141,14 +142,14 @@ def tile_routed_moe_kernel(tc, xT, w1, w2, gate, offs, out):
                 codes = place([P, width], U32, f"{name}_words", offset)
             exponents = keep.tile([P, width], U8, name=f"{name}_scales", align_bytes=64)
             nc.vector.quantize_mx(
-                out=codes[:].bitcast(FP8X4), scales=exponents[:], in_=grouped[:].rearrange("p c j -> p (c j)")
+                out=codes[:].bitcast(FP8X4), scales=exponents[:], in_=grouped.rearrange("p c j -> p (c j)")
             )
             return codes, exponents
 
         h_sums = {}
 
         def layer1(e, a, grouped):
-            w1_words, w1_scales = quantise(f"w1_{e}_{a}", grouped)
+            w1_words, w1_scales = quantise(f"w1_{e}_{a}", grouped[:])
             for u in range(BANKS):
                 if a == 0:
                     h_sums[e, u] = h_psum.tile([P, TILES, BANK_SLOTS], F32, name="h_sums")
@@ -188,22 +189,25 @@ def tile_routed_moe_kernel(tc, xT, w1, w2, gate, offs, out):
         def layer2(e, h_grouped, w2_grouped):
             held = BUFFER * (PASSES * (e + 1) + 1)
             if e < LAST:
-                h_words, h_scales = quantise(f"h_{e}", h_grouped, held)
-            w2_words, w2_scales = quantise(f"w2_{e}", w2_grouped, held + 4 * C if e == 0 else None)
+                parts = [(slice(0, C), quantise(f"h_{e}", h_grouped[:], held))]
+            w2_words, w2_scales = quantise(f"w2_{e}", w2_grouped[:], held + 4 * C if e == 0 else None)
             if e == LAST:
-                h_words, h_scales = quantise(f"h_{e}", h_grouped)
+                halves = [slice(BANK_SLOTS * u, BANK_SLOTS * (u + 1)) for u in range(BANKS)]
+                parts = [(slots, quantise(f"h_{e}_{u}", h_grouped[:, slots])) for u, slots in enumerate(halves)]
             for b in range(OUT_TILES):
-                features = slice(P * b, P * (b + 1))
                 y_sums[e, b] = y_psum.tile([P, C], F32, name="y_sums")
-                nc.tensor.matmul_mx(
-                    out=y_sums[e, b][:],
-                    lhsT=w2_words[:, features].bitcast(FP8X4),
-                    lhsT_scale=w2_scales[:, features],
-                    rhs=h_words[:].bitcast(FP8X4),
-                    rhs_scale=h_scales[:],
-                    start=True,
-                    stop=True,
-                )
+            for slots, (h_words, h_scales) in parts:
+                for b in range(OUT_TILES):
+                    features = slice(P * b, P * (b + 1))
+                    nc.tensor.matmul_mx(
+                        out=y_sums[e, b][:, slots],
+                        lhsT=w2_words[:, features].bitcast(FP8X4),
+                        lhsT_scale=w2_scales[:, features],
+                        rhs=h_words[:].bitcast(FP8X4),
+                        rhs_scale=h_scales[:],
+                        start=True,
+                        stop=True,
+                    )
 
         def apply_gate(e, b):
             gated = keep.tile([P, C], F32, name=f"gated{e}_{b}", align_bytes=64)

@@ -41,10 +41,10 @@ def interleave(copy, grouped, raw):
     )
 
 
-def interleave_w1(copy, grouped, raw, groups):
+def interleave_w1(copy, grouped, raw, groups, pair=slice(None)):
     copy(
-        grouped.rearrange("p (u v m) j -> p u m j v", u=TILES // PAIR, v=PAIR)[:, :, groups],
-        raw.rearrange("p j (m u v) -> p u m j v", u=TILES // PAIR, v=PAIR)[:, :, groups],
+        grouped.rearrange("p (u v m) j -> p u m j v", u=TILES // PAIR, v=PAIR)[:, pair, groups],
+        raw.rearrange("p j (m u v) -> p u m j v", u=TILES // PAIR, v=PAIR)[:, pair, groups],
     )
 
 
@@ -94,14 +94,19 @@ def tile_routed_moe_kernel(tc, xT, w1, w2, gate, offs, out):
         load_x(0)
         nc.sync.dma_start(slots_list[:], offs)
         load_x(1)
-        for e in range(E + 2):
+        for e in range(E):
             for a in range(PASSES):
-                if e < E:
-                    load_w1(e, a)
-                if e >= 2:
-                    load_gate(e - 2, a)
-                if 1 <= e <= E and a == (0 if e in (1, E) else 1):
+                load_w1(e, a)
+                if e >= 2 and a == 0:
+                    for b in range(OUT_TILES):
+                        load_gate(e - 2, b)
+                if e >= 1 and a == 1:
                     load_w2(e - 1)
+        load_gate(LAST - 1, 0)
+        load_w2(LAST)
+        load_gate(LAST - 1, 1)
+        load_gate(LAST, 0)
+        load_gate(LAST, 1)
 
         for b in range(OUT_TILES):
             nc.vector.memset(windows[b][:], 0.0)
@@ -122,16 +127,19 @@ def tile_routed_moe_kernel(tc, xT, w1, w2, gate, offs, out):
         def round_w1(e, a):
             grouped = x_pool.tile([P, H, PACK], BF16, name="w1_grouped", align_bytes=64)
             groups = P
-            scalar = groups if e == 0 else groups // 2 if (e, a) == (1, 0) else 0
+            scalar = groups if e == 0 else 3 * groups // 4 if (e, a) == (1, 0) else 0
             if scalar > 0:
                 interleave_w1(nc.scalar.copy, grouped[:], w1_raw[e, a][:], slice(0, scalar))
-            if scalar < groups:
+            if e > 0 and a == 1:
+                for pair in range(TILES // PAIR):
+                    interleave_w1(nc.vector.tensor_copy, grouped[:], w1_raw[e, a][:], slice(0, groups), pair)
+            elif scalar < groups:
                 interleave_w1(nc.vector.tensor_copy, grouped[:], w1_raw[e, a][:], slice(scalar, groups))
             return grouped
 
         def round_w2(e):
             grouped = h_pool.tile([P, N, PACK], BF16, name="w2_grouped", align_bytes=64)
-            interleave(nc.scalar.copy if e == 0 else nc.vector.tensor_copy, grouped[:], w2_raw[e][:])
+            interleave(nc.vector.tensor_copy, grouped[:], w2_raw[e][:])
             return grouped
 
         def quantise(name, grouped, offset=None):
@@ -149,13 +157,15 @@ def tile_routed_moe_kernel(tc, xT, w1, w2, gate, offs, out):
         h_sums = {}
 
         def layer1(e, a, grouped):
-            w1_words, w1_scales = quantise(f"w1_{e}_{a}", grouped[:])
+            step = H // PAIR if e > 0 and a == 1 else H
+            parts = [quantise(f"w1_{e}_{a}_{c}", grouped[:, c : c + step]) for c in range(0, H, step)]
             for u in range(BANKS):
                 if a == 0:
                     h_sums[e, u] = h_psum.tile([P, TILES, BANK_SLOTS], F32, name="h_sums")
                 slots = slice(C * e + BANK_SLOTS * u, C * e + BANK_SLOTS * (u + 1))
                 for t in range(TILES):
-                    columns = slice(P * t, P * (t + 1))
+                    w1_words, w1_scales = parts[P * t // step]
+                    columns = slice(P * t % step, P * t % step + P)
                     nc.tensor.matmul_mx(
                         out=h_sums[e, u][:, t],
                         lhsT=w1_words[:, columns].bitcast(FP8X4),
@@ -170,18 +180,11 @@ def tile_routed_moe_kernel(tc, xT, w1, w2, gate, offs, out):
             relu = flat.rearrange("p (u n t) -> p u n t", u=BANKS, t=TILES)
             grouped = h_pool.tile([P, C, PACK], BF16, name="h_grouped", align_bytes=64)
             halves = grouped[:].rearrange("p (u n) t -> p u n t", u=BANKS)
-            on_scalar = range(0 if e < LAST else 1, BANKS)
             for u in range(BANKS):
                 sums = h_sums[e, u][:].rearrange("p t n -> p n t")
-                if u in on_scalar:
-                    nc.scalar.activation(relu[:, u], sums, RELU)
-                else:
-                    nc.vector.tensor_scalar_max(relu[:, u], sums, 0.0)
+                nc.scalar.activation(relu[:, u], sums, RELU)
             for u in range(BANKS):
-                if u in on_scalar:
-                    nc.scalar.activation(halves[:, u], relu[:, u], SQUARE)
-                else:
-                    nc.vector.tensor_tensor(halves[:, u], relu[:, u], relu[:, u], MULT)
+                nc.scalar.activation(halves[:, u], relu[:, u], SQUARE)
             return grouped
 
         y_sums = {}
@@ -190,7 +193,7 @@ def tile_routed_moe_kernel(tc, xT, w1, w2, gate, offs, out):
             held = BUFFER * (PASSES * (e + 1) + 1)
             if e < LAST:
                 parts = [(slice(0, C), quantise(f"h_{e}", h_grouped[:], held))]
-            w2_words, w2_scales = quantise(f"w2_{e}", w2_grouped[:], held + 4 * C if e == 0 else None)
+            w2_words, w2_scales = quantise(f"w2_{e}", w2_grouped[:])
             if e == LAST:
                 halves = [slice(BANK_SLOTS * u, BANK_SLOTS * (u + 1)) for u in range(BANKS)]
                 parts = [(slots, quantise(f"h_{e}_{u}", h_grouped[:, slots])) for u, slots in enumerate(halves)]
@@ -226,26 +229,23 @@ def tile_routed_moe_kernel(tc, xT, w1, w2, gate, offs, out):
             nc.vector.tensor_copy(slot_words[a][:], words[a][:].indirect(slots_list[:]))
         nc.vector.tensor_copy(slot_scales[:], scales[:].indirect(slots_list[:]))
 
-        def spent(raw):
-            return raw[:].rearrange("p j c -> p (j c)")[:, : TILES * C]
-
         for a in range(PASSES):
             layer1(0, a, round_w1(0, a))
         layer1(1, 0, round_w1(1, 0))
-        w2_grouped = round_w2(0)
-        h_grouped = activate(0, spent(w2_raw[0]))
+        h_grouped = activate(0, h_pool.tile([P, TILES * C], F32, name="relu")[:])
         layer1(1, 1, round_w1(1, 1))
-        layer2(0, h_grouped, w2_grouped)
+        layer2(0, h_grouped, round_w2(0))
         for e in range(1, LAST):
             h_grouped = activate(e, h_pool.tile([P, TILES * C], F32, name="relu")[:])
-            for a in range(PASSES):
-                grouped = round_w1(e + 1, a)
-                scatter(e - 1, a, apply_gate(e - 1, a))
-                layer1(e + 1, a, grouped)
+            grouped = round_w1(e + 1, 0)
+            for b in range(OUT_TILES):
+                scatter(e - 1, b, apply_gate(e - 1, b))
+            layer1(e + 1, 0, grouped)
+            layer1(e + 1, 1, round_w1(e + 1, 1))
             layer2(e, h_grouped, round_w2(e))
-        w2_grouped = round_w2(LAST)
         h_grouped = activate(LAST, h_pool.tile([P, TILES * C], F32, name="relu")[:])
         scatter(LAST - 1, 0, apply_gate(LAST - 1, 0))
+        w2_grouped = round_w2(LAST)
         layer2(LAST, h_grouped, w2_grouped)
         scatter(LAST - 1, 1, apply_gate(LAST - 1, 1))
         gated = [apply_gate(LAST, b) for b in range(OUT_TILES)]

@@ -36,8 +36,8 @@ X_VECTOR = (9 * CHUNK // 16, 9 * CHUNK // 16, CHUNK // 2)
 
 def interleave(copy, grouped, raw):
     copy(
-        grouped.rearrange("p (c i) j -> p c j i", i=PAIR),
-        raw.rearrange("p j (c i) -> p c j i", i=PAIR),
+        grouped.rearrange("p (c i) j -> p c j i", i=PACK),
+        raw.rearrange("p j (c i) -> p c j i", i=PACK),
     )
 
 
@@ -184,7 +184,10 @@ def tile_routed_moe_kernel(tc, xT, w1, w2, gate, offs, out):
                 sums = h_sums[e, u][:].rearrange("p t n -> p n t")
                 nc.scalar.activation(relu[:, u], sums, RELU)
             for u in range(BANKS):
-                nc.scalar.activation(halves[:, u], relu[:, u], SQUARE)
+                if (e, u) == (LAST, BANKS - 1):
+                    nc.vector.tensor_tensor(halves[:, u], relu[:, u], relu[:, u], MULT)
+                else:
+                    nc.scalar.activation(halves[:, u], relu[:, u], SQUARE)
             return grouped
 
         y_sums = {}
@@ -243,8 +246,9 @@ def tile_routed_moe_kernel(tc, xT, w1, w2, gate, offs, out):
             layer1(e + 1, 0, grouped)
             layer1(e + 1, 1, round_w1(e + 1, 1))
             layer2(e, h_grouped, round_w2(e))
+        gated = apply_gate(LAST - 1, 0)
         h_grouped = activate(LAST, h_pool.tile([P, TILES * C], F32, name="relu")[:])
-        scatter(LAST - 1, 0, apply_gate(LAST - 1, 0))
+        scatter(LAST - 1, 0, gated)
         w2_grouped = round_w2(LAST)
         layer2(LAST, h_grouped, w2_grouped)
         scatter(LAST - 1, 1, apply_gate(LAST - 1, 1))

@@ -117,17 +117,19 @@ def tile_routed_moe_kernel(tc, xT, w1, w2, gate, offs, out):
                 share = X_VECTOR[c]
                 interleave(nc.vector.tensor_copy, grouped[:, :share], raw[:, :, :share])
                 interleave(nc.scalar.copy, grouped[:, share:], raw[:, :, share:])
-                tokens = slice(c * CHUNK, (c + 1) * CHUNK)
-                nc.vector.quantize_mx(
-                    out=words[a][:, tokens].bitcast(FP8X4),
-                    scales=scales[SCALE_ROWS * a : P, tokens],
-                    in_=grouped[:].rearrange("p c j -> p (c j)"),
-                )
+                step = share if (a, c) == (PASSES - 1, T // CHUNK - 1) else CHUNK
+                for first in range(0, CHUNK, step):
+                    tokens = slice(c * CHUNK + first, c * CHUNK + first + step)
+                    nc.vector.quantize_mx(
+                        out=words[a][:, tokens].bitcast(FP8X4),
+                        scales=scales[SCALE_ROWS * a : P, tokens],
+                        in_=grouped[:, first : first + step].rearrange("p c j -> p (c j)"),
+                    )
 
         def round_w1(e, a):
             grouped = x_pool.tile([P, H, PACK], BF16, name="w1_grouped", align_bytes=64)
             groups = P
-            scalar = groups if e == 0 else 3 * groups // 4 if (e, a) == (1, 0) else 0
+            scalar = groups if e == 0 else 5 * groups // 8 if (e, a) == (1, 0) else 0
             if scalar > 0:
                 interleave_w1(nc.scalar.copy, grouped[:], w1_raw[e, a][:], slice(0, scalar))
             if e > 0 and a == 1:

@@ -31,6 +31,7 @@ CHUNK = 512
 LONG = 2 * CHUNK
 BUFFER = PACK * H * 4
 LAST = E - 1
+HANDED = 32
 X_VECTOR = (9 * CHUNK // 16, 9 * CHUNK // 16, CHUNK // 2)
 
 
@@ -141,7 +142,10 @@ def tile_routed_moe_kernel(tc, xT, w1, w2, gate, offs, out):
 
         def round_w2(e):
             grouped = h_pool.tile([P, N, PACK], BF16, name="w2_grouped", align_bytes=64)
-            interleave(nc.vector.tensor_copy, grouped[:], w2_raw[e][:])
+            step = P if e == LAST - 1 else N
+            for first in range(0, N, step):
+                features = slice(first, first + step)
+                interleave(nc.vector.tensor_copy, grouped[:, features], w2_raw[e][:, :, features])
             return grouped
 
         def quantise(name, grouped, offset=None):
@@ -195,10 +199,11 @@ def tile_routed_moe_kernel(tc, xT, w1, w2, gate, offs, out):
         y_sums = {}
 
         def layer2(e, h_grouped, w2_grouped):
-            held = BUFFER * (PASSES * (e + 1) + 1)
+            held = BUFFER * (PASSES * (e + 1) + (0 if e == LAST - 1 else 1))
             if e < LAST:
                 parts = [(slice(0, C), quantise(f"h_{e}", h_grouped[:], held))]
-            w2_words, w2_scales = quantise(f"w2_{e}", w2_grouped[:])
+            step = P if e == LAST - 1 else N
+            w2_mx = [quantise(f"w2_{e}_{c}", w2_grouped[:, c : c + step]) for c in range(0, N, step)]
             if e == LAST:
                 halves = [slice(BANK_SLOTS * u, BANK_SLOTS * (u + 1)) for u in range(BANKS)]
                 parts = [(slots, quantise(f"h_{e}_{u}", h_grouped[:, slots])) for u, slots in enumerate(halves)]
@@ -206,7 +211,8 @@ def tile_routed_moe_kernel(tc, xT, w1, w2, gate, offs, out):
                 y_sums[e, b] = y_psum.tile([P, C], F32, name="y_sums")
             for slots, (h_words, h_scales) in parts:
                 for b in range(OUT_TILES):
-                    features = slice(P * b, P * (b + 1))
+                    w2_words, w2_scales = w2_mx[P * b // step]
+                    features = slice(P * b % step, P * b % step + P)
                     nc.tensor.matmul_mx(
                         out=y_sums[e, b][:, slots],
                         lhsT=w2_words[:, features].bitcast(FP8X4),
@@ -217,17 +223,19 @@ def tile_routed_moe_kernel(tc, xT, w1, w2, gate, offs, out):
                         stop=True,
                     )
 
-        def apply_gate(e, b):
-            gated = keep.tile([P, C], F32, name=f"gated{e}_{b}", align_bytes=64)
-            nc.vector.tensor_tensor(gated[:], y_sums[e, b][:], gate_sb[e, b][:], MULT)
-            return gated
+        gated = [keep.tile([P, E * C], F32, name=f"gated{b}", align_bytes=64) for b in range(OUT_TILES)]
 
-        def scatter(e, b, gated):
-            window = windows[b][:].indirect(slots_list[:, C // LIST_ROWS * e : C // LIST_ROWS * (e + 1)])
+        def apply_gate(e, b):
+            nc.vector.tensor_tensor(gated[b][:, C * e : C * (e + 1)], y_sums[e, b][:], gate_sb[e, b][:], MULT)
+
+        def scatter(e, b):
+            first = C * e - (HANDED if (e, b) == (LAST, 0) else 0)
+            end = C * (e + 1) - (HANDED if (e, b) == (LAST - 1, 0) else 0)
+            window = windows[b][:].indirect(slots_list[:, first // LIST_ROWS : end // LIST_ROWS])
             if (e, b) == (LAST, 0):
-                nc.vector.tensor_copy(window, gated[:])
+                nc.vector.tensor_copy(window, gated[b][:, first:end])
             else:
-                nc.scalar.activation(window, gated[:], COPY)
+                nc.scalar.activation(window, gated[b][:, first:end], COPY)
 
         for a in range(PASSES):
             quantise_x(a)
@@ -244,19 +252,22 @@ def tile_routed_moe_kernel(tc, xT, w1, w2, gate, offs, out):
             h_grouped = activate(e, h_pool.tile([P, TILES * C], F32, name="relu")[:])
             grouped = round_w1(e + 1, 0)
             for b in range(OUT_TILES):
-                scatter(e - 1, b, apply_gate(e - 1, b))
+                apply_gate(e - 1, b)
+                scatter(e - 1, b)
             layer1(e + 1, 0, grouped)
             layer1(e + 1, 1, round_w1(e + 1, 1))
             layer2(e, h_grouped, round_w2(e))
-        gated = apply_gate(LAST - 1, 0)
+        apply_gate(LAST - 1, 0)
         h_grouped = activate(LAST, h_pool.tile([P, TILES * C], F32, name="relu")[:])
-        scatter(LAST - 1, 0, gated)
+        scatter(LAST - 1, 0)
         w2_grouped = round_w2(LAST)
         layer2(LAST, h_grouped, w2_grouped)
-        scatter(LAST - 1, 1, apply_gate(LAST - 1, 1))
-        gated = [apply_gate(LAST, b) for b in range(OUT_TILES)]
+        apply_gate(LAST - 1, 1)
+        scatter(LAST - 1, 1)
         for b in range(OUT_TILES):
-            scatter(LAST, b, gated[b])
+            apply_gate(LAST, b)
+        for b in range(OUT_TILES):
+            scatter(LAST, b)
 
         for b in range(OUT_TILES):
             nc.sync.dma_start(out[P * b : P * (b + 1), :], windows[b][:])

@@ -31,7 +31,7 @@ CHUNK = 512
 LONG = 2 * CHUNK
 BUFFER = PACK * H * 4
 LAST = E - 1
-HANDED = 32
+HANDED = 64
 X_VECTOR = (9 * CHUNK // 16, 9 * CHUNK // 16, CHUNK // 2)
 
 
@@ -103,8 +103,8 @@ def tile_routed_moe_kernel(tc, xT, w1, w2, gate, offs, out):
                         load_gate(e - 2, b)
                 if e >= 1 and a == 1:
                     load_w2(e - 1)
-        load_gate(LAST - 1, 0)
         load_w2(LAST)
+        load_gate(LAST - 1, 0)
         load_gate(LAST - 1, 1)
         load_gate(LAST, 0)
         load_gate(LAST, 1)
@@ -183,17 +183,19 @@ def tile_routed_moe_kernel(tc, xT, w1, w2, gate, offs, out):
                     )
 
         def activate(e, flat):
-            relu = flat.rearrange("p (u n t) -> p u n t", u=BANKS, t=TILES)
+            relu = flat.rearrange("p (n t) -> p n t", t=TILES)
             grouped = h_pool.tile([P, C, PACK], BF16, name="h_grouped", align_bytes=64)
-            halves = grouped[:].rearrange("p (u n) t -> p u n t", u=BANKS)
-            for u in range(BANKS):
-                sums = h_sums[e, u][:].rearrange("p t n -> p n t")
-                nc.scalar.activation(relu[:, u], sums, RELU)
-            for u in range(BANKS):
-                if (e, u) == (LAST, BANKS - 1):
-                    nc.vector.tensor_tensor(halves[:, u], relu[:, u], relu[:, u], MULT)
+            banks = [(u, slice(0, BANK_SLOTS)) for u in range(BANKS)]
+            if e == LAST:
+                banks[-1:] = [(BANKS - 1, slice(n, n + BANK_SLOTS // 2)) for n in (0, BANK_SLOTS // 2)]
+            places = [slice(BANK_SLOTS * u + part.start, BANK_SLOTS * u + part.stop) for u, part in banks]
+            for (u, part), slots in zip(banks, places):
+                nc.scalar.activation(relu[:, slots], h_sums[e, u][:].rearrange("p t n -> p n t")[:, part], RELU)
+            for (u, part), slots in zip(banks, places):
+                if (e, u) == (LAST, 0):
+                    nc.vector.tensor_tensor(grouped[:, slots], relu[:, slots], relu[:, slots], MULT)
                 else:
-                    nc.scalar.activation(halves[:, u], relu[:, u], SQUARE)
+                    nc.scalar.activation(grouped[:, slots], relu[:, slots], SQUARE)
             return grouped
 
         y_sums = {}

@@ -26,13 +26,14 @@ BANK_SLOTS = 128
 BANKS = C // BANK_SLOTS
 OUT_TILES = N // P
 LIST_ROWS = 16
-SCALE_ROWS = 4
-CHUNK = 512
-LONG = 2 * CHUNK
+SLOTS = E * C
+PLANE = T * 4
 BUFFER = PACK * H * 4
 LAST = E - 1
 HANDED = 64
-X_VECTOR = (9 * CHUNK // 16, 9 * CHUNK // 16, CHUNK // 2)
+STEPPED = (512, 0)
+X_VECTOR = (512, 512, 512, 512, 352, 352, 352, 512)
+W1_SCALAR = {(0, 0): 128, (0, 1): 80, (1, 0): 64}
 
 
 def interleave(copy, grouped, raw):
@@ -63,22 +64,28 @@ def tile_routed_moe_kernel(tc, xT, w1, w2, gate, offs, out):
             return placed.tile(shape, dtype, name=name, align_bytes=64, offset=offset)
 
         slots_list = keep.tile([P, E * C // LIST_ROWS], U16, name="slots_list", align_bytes=64)
-        words = [keep.tile([P, T], U32, name=f"words{a}", align_bytes=64) for a in range(PASSES)]
-        scales = keep.tile([P, T], U8, name="scales", align_bytes=64)
-        nc.gpsimd.memset(scales[:], 0)
-        slot_words = [keep.tile([P, E * C], U32, name=f"slot_words{a}", align_bytes=64) for a in range(PASSES)]
-        slot_scales = keep.tile([P, E * C], U8, name="slot_scales", align_bytes=64)
+        picked = [keep.tile([P, PACK, SLOTS], F32, name=f"picked{a}", align_bytes=64) for a in range(PASSES)]
+        x_grouped = [keep.tile([P, SLOTS, PACK], BF16, name=f"x_grouped{a}", align_bytes=64) for a in range(PASSES)]
+        slot_words = [keep.tile([P, SLOTS], U32, name=f"slot_words{a}", align_bytes=64) for a in range(PASSES)]
+        slot_scales = [keep.tile([P, SLOTS], U8, name=f"slot_scales{a}", align_bytes=64) for a in range(PASSES)]
         windows = [keep.tile([P, T], F32, name=f"window{b}", align_bytes=64) for b in range(OUT_TILES)]
 
         x_raw, w1_raw, w2_raw, gate_sb = {}, {}, {}, {}
 
-        def load_x(a):
-            rows = xT.rearrange("(a p j) n -> a p j n", p=P, j=PACK)[a]
-            long = keep.tile([P, PACK, LONG], F32, name=f"x_long{a}", align_bytes=64)
-            nc.sync.dma_start(long[:], rows[:, :, :LONG])
-            short = place([P, PACK, T - LONG], F32, f"x_short{a}", BUFFER * (HALVES - PASSES + a))
-            nc.sync.dma_start(short[:], rows[:, :, LONG:])
-            x_raw[a] = [long[:, :, :CHUNK], long[:, :, CHUNK:], short[:]]
+        def offsets(first, end):
+            return slots_list[:, first // LIST_ROWS : end // LIST_ROWS]
+
+        def load_plane(a, j):
+            x_raw[a, j] = place([P, T], F32, f"plane{a}_{j}", PASSES * BUFFER + PLANE * (PACK * a + j))
+            nc.sync.dma_start(x_raw[a, j][:], xT.rearrange("(a p j) n -> a j p n", p=P, j=PACK)[a, j])
+
+        def gather_plane(a, j):
+            stepped, share = STEPPED[a], X_VECTOR[PACK * a + j]
+            if stepped > 0:
+                nc.vector.tensor_copy(x_grouped[a][:, :stepped, j], x_raw[a, j][:].indirect(offsets(0, stepped)))
+            if share > stepped:
+                nc.vector.tensor_copy(picked[a][:, j, stepped:share], x_raw[a, j][:].indirect(offsets(stepped, share)))
+            nc.scalar.activation(picked[a][:, j, share:], x_raw[a, j][:].indirect(offsets(share, SLOTS)), COPY)
 
         def load_w1(e, a):
             w1_raw[e, a] = place([P, PACK, H], F32, f"w1_raw{e}_{a}", BUFFER * (PASSES * e + a))
@@ -92,9 +99,13 @@ def tile_routed_moe_kernel(tc, xT, w1, w2, gate, offs, out):
             gate_sb[e, b] = keep.tile([P, C], F32, name=f"gate_sb{e}_{b}", align_bytes=64)
             nc.sync.dma_start(gate_sb[e, b][:], gate[P * b : P * (b + 1), C * e : C * (e + 1)])
 
-        load_x(0)
+        for b in range(OUT_TILES):
+            nc.vector.memset(windows[b][:], 0.0)
         nc.sync.dma_start(slots_list[:], offs)
-        load_x(1)
+        for a in range(PASSES):
+            for j in range(PACK):
+                load_plane(a, j)
+                gather_plane(a, j)
         for e in range(E):
             for a in range(PASSES):
                 load_w1(e, a)
@@ -109,33 +120,35 @@ def tile_routed_moe_kernel(tc, xT, w1, w2, gate, offs, out):
         load_gate(LAST, 0)
         load_gate(LAST, 1)
 
-        for b in range(OUT_TILES):
-            nc.vector.memset(windows[b][:], 0.0)
+        def round_x(a, first, end, copy):
+            interleave(copy, x_grouped[a][:, first:end], picked[a][:, :, first:end])
 
-        def quantise_x(a):
-            for c, raw in enumerate(x_raw[a]):
-                grouped = x_pool.tile([P, CHUNK, PACK], BF16, name="x_grouped", align_bytes=64)
-                share = X_VECTOR[c]
-                interleave(nc.vector.tensor_copy, grouped[:, :share], raw[:, :, :share])
-                interleave(nc.scalar.copy, grouped[:, share:], raw[:, :, share:])
-                step = share if (a, c) == (PASSES - 1, T // CHUNK - 1) else CHUNK
-                for first in range(0, CHUNK, step):
-                    tokens = slice(c * CHUNK + first, c * CHUNK + first + step)
-                    nc.vector.quantize_mx(
-                        out=words[a][:, tokens].bitcast(FP8X4),
-                        scales=scales[SCALE_ROWS * a : P, tokens],
-                        in_=grouped[:, first : first + step].rearrange("p c j -> p (c j)"),
-                    )
+        def quantise_x(a, first, end):
+            nc.vector.quantize_mx(
+                out=slot_words[a][:, first:end].bitcast(FP8X4),
+                scales=slot_scales[a][:, first:end],
+                in_=x_grouped[a][:, first:end].rearrange("p c j -> p (c j)"),
+            )
+
+        middle = (STEPPED[0] + SLOTS) // 2
+        round_x(0, STEPPED[0], middle, nc.vector.tensor_copy)
+        round_x(0, middle, SLOTS, nc.vector.tensor_copy)
+        quantise_x(0, 0, 2 * C)
+        quantise_x(0, 2 * C, SLOTS)
+        for e in range(E):
+            round_x(1, C * e, C * (e + 1), nc.scalar.copy if e == LAST else nc.vector.tensor_copy)
+            if e % 2 == 1:
+                quantise_x(1, C * (e - 1), C * (e + 1))
 
         def round_w1(e, a):
             grouped = x_pool.tile([P, H, PACK], BF16, name="w1_grouped", align_bytes=64)
             groups = P
-            scalar = groups if e == 0 else 5 * groups // 8 if (e, a) == (1, 0) else 0
+            scalar = W1_SCALAR.get((e, a), 0)
             if scalar > 0:
                 interleave_w1(nc.scalar.copy, grouped[:], w1_raw[e, a][:], slice(0, scalar))
             if e > 0 and a == 1:
                 for pair in range(TILES // PAIR):
-                    interleave_w1(nc.vector.tensor_copy, grouped[:], w1_raw[e, a][:], slice(0, groups), pair)
+                    interleave_w1(nc.vector.tensor_copy, grouped[:], w1_raw[e, a][:], slice(scalar, groups), pair)
             elif scalar < groups:
                 interleave_w1(nc.vector.tensor_copy, grouped[:], w1_raw[e, a][:], slice(scalar, groups))
             return grouped
@@ -177,7 +190,7 @@ def tile_routed_moe_kernel(tc, xT, w1, w2, gate, offs, out):
                         lhsT=w1_words[:, columns].bitcast(FP8X4),
                         lhsT_scale=w1_scales[:, columns],
                         rhs=slot_words[a][:, slots].bitcast(FP8X4),
-                        rhs_scale=slot_scales[SCALE_ROWS * a : P, slots],
+                        rhs_scale=slot_scales[a][:, slots],
                         start=(a == 0 and t == 0),
                         stop=(a == PASSES - 1 and t == TILES - 1),
                     )
@@ -238,11 +251,6 @@ def tile_routed_moe_kernel(tc, xT, w1, w2, gate, offs, out):
                 nc.vector.tensor_copy(window, gated[b][:, first:end])
             else:
                 nc.scalar.activation(window, gated[b][:, first:end], COPY)
-
-        for a in range(PASSES):
-            quantise_x(a)
-            nc.vector.tensor_copy(slot_words[a][:], words[a][:].indirect(slots_list[:]))
-        nc.vector.tensor_copy(slot_scales[:], scales[:].indirect(slots_list[:]))
 
         for a in range(PASSES):
             layer1(0, a, round_w1(0, a))

@@ -31,9 +31,9 @@ PLANE = T * 4
 BUFFER = PACK * H * 4
 LAST = E - 1
 HANDED = 64
-STEPPED = (512, 0)
-X_VECTOR = (512, 512, 512, 512, 352, 352, 352, 512)
-W1_SCALAR = {(0, 0): 128, (0, 1): 80, (1, 0): 64}
+STEPPED = (384, 0)
+X_VECTOR = (384, 384, 384, 384, 320, 320, 320, 512)
+W1_SCALAR = {(0, 0): 64, (0, 1): 48, (1, 0): 48}
 
 
 def interleave(copy, grouped, raw):
@@ -99,8 +99,8 @@ def tile_routed_moe_kernel(tc, xT, w1, w2, gate, offs, out):
             gate_sb[e, b] = keep.tile([P, C], F32, name=f"gate_sb{e}_{b}", align_bytes=64)
             nc.sync.dma_start(gate_sb[e, b][:], gate[P * b : P * (b + 1), C * e : C * (e + 1)])
 
-        for b in range(OUT_TILES):
-            nc.vector.memset(windows[b][:], 0.0)
+        nc.vector.memset(windows[0][:], 0.0)
+        nc.scalar.copy(windows[1][:], windows[0][:])
         nc.sync.dma_start(slots_list[:], offs)
         for a in range(PASSES):
             for j in range(PACK):
@@ -136,7 +136,7 @@ def tile_routed_moe_kernel(tc, xT, w1, w2, gate, offs, out):
         quantise_x(0, 0, 2 * C)
         quantise_x(0, 2 * C, SLOTS)
         for e in range(E):
-            round_x(1, C * e, C * (e + 1), nc.scalar.copy if e == LAST else nc.vector.tensor_copy)
+            round_x(1, C * e, C * (e + 1), nc.scalar.copy if e >= E // 2 else nc.vector.tensor_copy)
             if e % 2 == 1:
                 quantise_x(1, C * (e - 1), C * (e + 1))
 
@@ -255,7 +255,7 @@ def tile_routed_moe_kernel(tc, xT, w1, w2, gate, offs, out):
         for a in range(PASSES):
             layer1(0, a, round_w1(0, a))
         layer1(1, 0, round_w1(1, 0))
-        h_grouped = activate(0, h_pool.tile([P, TILES * C], F32, name="relu")[:])
+        h_grouped = activate(0, place([P, TILES * C], F32, "first_relu", BUFFER * PASSES)[:])
         layer1(1, 1, round_w1(1, 1))
         layer2(0, h_grouped, round_w2(0))
         for e in range(1, LAST):

@@ -196,19 +196,22 @@ def tile_routed_moe_kernel(tc, xT, w1, w2, gate, offs, out):
                     )
 
         def activate(e, flat):
-            relu = flat.rearrange("p (n t) -> p n t", t=TILES)
+            relu = flat.rearrange("p (m t s) -> p m t s", t=TILES, s=PAIR)
             grouped = h_pool.tile([P, C, PACK], BF16, name="h_grouped", align_bytes=64)
             banks = [(u, slice(0, BANK_SLOTS)) for u in range(BANKS)]
             if e == LAST:
                 banks[-1:] = [(BANKS - 1, slice(n, n + BANK_SLOTS // 2)) for n in (0, BANK_SLOTS // 2)]
             places = [slice(BANK_SLOTS * u + part.start, BANK_SLOTS * u + part.stop) for u, part in banks]
             for (u, part), slots in zip(banks, places):
-                nc.scalar.activation(relu[:, slots], h_sums[e, u][:].rearrange("p t n -> p n t")[:, part], RELU)
+                sums = h_sums[e, u][:, :, part].rearrange("p t (m s) -> p m t s", s=PAIR)
+                nc.scalar.activation(relu[:, slots.start // PAIR : slots.stop // PAIR], sums, RELU)
             for (u, part), slots in zip(banks, places):
+                values = relu[:, slots.start // PAIR : slots.stop // PAIR].rearrange("p m t s -> p m s t")
+                words = grouped[:, slots].rearrange("p (m s) t -> p m s t", s=PAIR)
                 if (e, u) == (LAST, 0):
-                    nc.vector.tensor_tensor(grouped[:, slots], relu[:, slots], relu[:, slots], MULT)
+                    nc.vector.tensor_tensor(words, values, values, MULT)
                 else:
-                    nc.scalar.activation(grouped[:, slots], relu[:, slots], SQUARE)
+                    nc.scalar.activation(words, values, SQUARE)
             return grouped
 
         y_sums = {}

@@ -30,7 +30,7 @@ SLOTS = E * C
 PLANE = T * 4
 BUFFER = PACK * H * 4
 LAST = E - 1
-HANDED = 64
+HANDED = 32
 STEPPED = (384, 0)
 X_VECTOR = (384, 384, 384, 384, 320, 320, 320, 512)
 W1_SCALAR = {(0, 0): 64, (0, 1): 48, (1, 0): 48}

@@ -7,6 +7,7 @@ FLOPS = 2 * E * C * (K * H + H * N)
 
 F32 = mybir.dt.float32
 BF16 = mybir.dt.bfloat16
+I32 = mybir.dt.int32
 U32 = mybir.dt.uint32
 U16 = mybir.dt.uint16
 U8 = mybir.dt.uint8
@@ -20,20 +21,18 @@ P = 128
 PACK = 4
 PAIR = 2
 PASSES = K // (P * PACK)
-HALVES = E * PASSES
 TILES = H // P
 BANK_SLOTS = 128
 BANKS = C // BANK_SLOTS
 OUT_TILES = N // P
 LIST_ROWS = 16
 SLOTS = E * C
-PLANE = T * 4
+ROWS = PAIR * T * 4
 BUFFER = PACK * H * 4
+ALIGN = 256
 LAST = E - 1
 HANDED = 32
-STEPPED = (384, 0)
-X_VECTOR = (384, 384, 384, 384, 320, 320, 320, 512)
-W1_SCALAR = {(0, 0): 64, (0, 1): 48, (1, 0): 48}
+W1_SCALAR = {(0, 0): 128, (0, 1): 48, (1, 0): 48}
 
 
 def interleave(copy, grouped, raw):
@@ -43,11 +42,17 @@ def interleave(copy, grouped, raw):
     )
 
 
-def interleave_w1(copy, grouped, raw, groups, pair=slice(None)):
-    copy(
-        grouped.rearrange("p (u v m) j -> p u m j v", u=TILES // PAIR, v=PAIR)[:, pair, groups],
-        raw.rearrange("p j (m u v) -> p u m j v", u=TILES // PAIR, v=PAIR)[:, pair, groups],
-    )
+def interleave_w1(copy, grouped, raw, groups, pair=None):
+    if pair is None:
+        copy(
+            grouped.rearrange("p (t m) (s r) -> p m s r t", t=TILES, s=PAIR)[:, groups],
+            raw.rearrange("p (r s) (m t) -> p m s r t", t=TILES, s=PAIR)[:, groups],
+        )
+    else:
+        copy(
+            grouped.rearrange("p (u v m) (s r) -> p u m s r v", u=TILES // PAIR, v=PAIR, s=PAIR)[:, pair, groups],
+            raw.rearrange("p (r s) (m u v) -> p u m s r v", u=TILES // PAIR, v=PAIR, s=PAIR)[:, pair, groups],
+        )
 
 
 def tile_routed_moe_kernel(tc, xT, w1, w2, gate, offs, out):
@@ -61,51 +66,41 @@ def tile_routed_moe_kernel(tc, xT, w1, w2, gate, offs, out):
         y_psum = ctx.enter_context(tc.psum_pool(name="y_psum", bufs=2 * OUT_TILES))
 
         def place(shape, dtype, name, offset):
-            return placed.tile(shape, dtype, name=name, align_bytes=64, offset=offset)
+            return placed.tile(shape, dtype, name=name, align_bytes=ALIGN, offset=offset)
 
-        slots_list = keep.tile([P, E * C // LIST_ROWS], U16, name="slots_list", align_bytes=64)
-        picked = [keep.tile([P, PACK, SLOTS], F32, name=f"picked{a}", align_bytes=64) for a in range(PASSES)]
-        x_grouped = [keep.tile([P, SLOTS, PACK], BF16, name=f"x_grouped{a}", align_bytes=64) for a in range(PASSES)]
+        slots_list = keep.tile([P, SLOTS // LIST_ROWS], U16, name="slots_list", align_bytes=64)
+        pairs = [keep.tile([P, PAIR, SLOTS, PAIR], BF16, name=f"pairs{a}", align_bytes=64) for a in range(PASSES)]
+        x_grouped = [keep.tile([P, SLOTS * PACK], BF16, name=f"x_grouped{a}", align_bytes=64) for a in range(PASSES)]
         slot_words = [keep.tile([P, SLOTS], U32, name=f"slot_words{a}", align_bytes=64) for a in range(PASSES)]
         slot_scales = [keep.tile([P, SLOTS], U8, name=f"slot_scales{a}", align_bytes=64) for a in range(PASSES)]
-        windows = [keep.tile([P, T], F32, name=f"window{b}", align_bytes=64) for b in range(OUT_TILES)]
+        windows = [keep.tile([P, T], F32, name=f"window{b}", align_bytes=ALIGN) for b in range(OUT_TILES)]
 
-        x_raw, w1_raw, w2_raw, gate_sb = {}, {}, {}, {}
+        w1_raw, w2_raw, gate_sb = {}, {}, {}
 
-        def offsets(first, end):
-            return slots_list[:, first // LIST_ROWS : end // LIST_ROWS]
-
-        def load_plane(a, j):
-            x_raw[a, j] = place([P, T], F32, f"plane{a}_{j}", PASSES * BUFFER + PLANE * (PACK * a + j))
-            nc.sync.dma_start(x_raw[a, j][:], xT.rearrange("(a p j) n -> a j p n", p=P, j=PACK)[a, j])
-
-        def gather_plane(a, j):
-            stepped, share = STEPPED[a], X_VECTOR[PACK * a + j]
-            if stepped > 0:
-                nc.vector.tensor_copy(x_grouped[a][:, :stepped, j], x_raw[a, j][:].indirect(offsets(0, stepped)))
-            if share > stepped:
-                nc.vector.tensor_copy(picked[a][:, j, stepped:share], x_raw[a, j][:].indirect(offsets(stepped, share)))
-            nc.scalar.activation(picked[a][:, j, share:], x_raw[a, j][:].indirect(offsets(share, SLOTS)), COPY)
+        def gather_rows(a, r):
+            rows = place([P, PAIR * T], F32, f"rows{a}_{r}", PASSES * BUFFER + ROWS * (PAIR * a + r))
+            nc.sync.dma_start(rows[:], xT.rearrange("(a p r s) n -> a r p (s n)", p=P, r=PAIR, s=PAIR)[a, r])
+            nc.scalar.activation(pairs[a][:, 0, :, r], rows[:].indirect(slots_list[:]), COPY)
+            nc.vector.tensor_copy(pairs[a][:, 1, :, r], rows[:, T:].indirect(slots_list[:]))
 
         def load_w1(e, a):
             w1_raw[e, a] = place([P, PACK, H], F32, f"w1_raw{e}_{a}", BUFFER * (PASSES * e + a))
             nc.sync.dma_start(w1_raw[e, a][:], w1[e].rearrange("(a p j) h -> a p j h", p=P, j=PACK)[a])
 
         def load_w2(e):
-            w2_raw[e] = keep.tile([P, PACK, N], F32, name=f"w2_raw{e}", align_bytes=64)
+            w2_raw[e] = keep.tile([P, PACK, N], F32, name=f"w2_raw{e}", align_bytes=ALIGN)
             nc.sync.dma_start(w2_raw[e][:], w2[e].rearrange("(p t) n -> p t n", t=PACK))
 
         def load_gate(e, b):
-            gate_sb[e, b] = keep.tile([P, C], F32, name=f"gate_sb{e}_{b}", align_bytes=64)
+            gate_sb[e, b] = keep.tile([P, C], F32, name=f"gate_sb{e}_{b}", align_bytes=ALIGN)
             nc.sync.dma_start(gate_sb[e, b][:], gate[P * b : P * (b + 1), C * e : C * (e + 1)])
 
         nc.vector.memset(windows[0][:], 0.0)
         nc.scalar.copy(windows[1][:], windows[0][:])
         nc.sync.dma_start(slots_list[:], offs)
         for a in range(PASSES):
-            for j in range(PACK):
-                load_plane(a, j)
-                gather_plane(a, j)
+            for r in range(PAIR):
+                gather_rows(a, r)
         for e in range(E):
             for a in range(PASSES):
                 load_w1(e, a)
@@ -115,30 +110,30 @@ def tile_routed_moe_kernel(tc, xT, w1, w2, gate, offs, out):
                 if e >= 1 and a == 1:
                     load_w2(e - 1)
         load_w2(LAST)
-        load_gate(LAST - 1, 0)
-        load_gate(LAST - 1, 1)
-        load_gate(LAST, 0)
-        load_gate(LAST, 1)
+        for e in (LAST - 1, LAST):
+            for b in range(OUT_TILES):
+                load_gate(e, b)
 
-        def round_x(a, first, end, copy):
-            interleave(copy, x_grouped[a][:, first:end], picked[a][:, :, first:end])
+        def join_x(a, first, end, copy, word):
+            joined = x_grouped[a][:].bitcast(word).rearrange("p (c s) -> p c s", s=PAIR)
+            halves = pairs[a][:].rearrange("p s c r -> p s (c r)").bitcast(word).rearrange("p s c -> p c s")
+            copy(joined[:, first:end], halves[:, first:end])
 
         def quantise_x(a, first, end):
             nc.vector.quantize_mx(
                 out=slot_words[a][:, first:end].bitcast(FP8X4),
                 scales=slot_scales[a][:, first:end],
-                in_=x_grouped[a][:, first:end].rearrange("p c j -> p (c j)"),
+                in_=x_grouped[a][:, PACK * first : PACK * end],
             )
 
-        middle = (STEPPED[0] + SLOTS) // 2
-        round_x(0, STEPPED[0], middle, nc.vector.tensor_copy)
-        round_x(0, middle, SLOTS, nc.vector.tensor_copy)
-        quantise_x(0, 0, 2 * C)
-        quantise_x(0, 2 * C, SLOTS)
-        for e in range(E):
-            round_x(1, C * e, C * (e + 1), nc.scalar.copy if e >= E // 2 else nc.vector.tensor_copy)
-            if e % 2 == 1:
-                quantise_x(1, C * (e - 1), C * (e + 1))
+        for a in range(PASSES):
+            for first in range(0, SLOTS, 2 * C):
+                if a == 0 and first > 0:
+                    join_x(a, first, first + 2 * C, nc.scalar.copy, U32)
+                else:
+                    join_x(a, first, first + 2 * C, nc.vector.tensor_copy, I32)
+            for first in range(0, SLOTS, 2 * C):
+                quantise_x(a, first, first + 2 * C)
 
         def round_w1(e, a):
             grouped = x_pool.tile([P, H, PACK], BF16, name="w1_grouped", align_bytes=64)

@@ -27,12 +27,14 @@ BANKS = C // BANK_SLOTS
 OUT_TILES = N // P
 LIST_ROWS = 16
 SLOTS = E * C
-ROWS = PAIR * T * 4
+GROUP = 2 * C
+PLANE = T * 4
+X_VECTOR = 448
 BUFFER = PACK * H * 4
 ALIGN = 256
 LAST = E - 1
 HANDED = 32
-W1_SCALAR = {(0, 0): 128, (0, 1): 48, (1, 0): 48}
+W1_SCALAR = {(0, 0): 80, (0, 1): 56, (1, 1): 64}
 
 
 def interleave(copy, grouped, raw):
@@ -42,17 +44,11 @@ def interleave(copy, grouped, raw):
     )
 
 
-def interleave_w1(copy, grouped, raw, groups, pair=None):
-    if pair is None:
-        copy(
-            grouped.rearrange("p (t m) (s r) -> p m s r t", t=TILES, s=PAIR)[:, groups],
-            raw.rearrange("p (r s) (m t) -> p m s r t", t=TILES, s=PAIR)[:, groups],
-        )
-    else:
-        copy(
-            grouped.rearrange("p (u v m) (s r) -> p u m s r v", u=TILES // PAIR, v=PAIR, s=PAIR)[:, pair, groups],
-            raw.rearrange("p (r s) (m u v) -> p u m s r v", u=TILES // PAIR, v=PAIR, s=PAIR)[:, pair, groups],
-        )
+def interleave_w1(copy, grouped, raw, groups, pair=slice(None)):
+    copy(
+        grouped.rearrange("p (u v m) j -> p u m j v", u=TILES // PAIR, v=PAIR)[:, pair, groups],
+        raw.rearrange("p j (m u v) -> p u m j v", u=TILES // PAIR, v=PAIR)[:, pair, groups],
+    )
 
 
 def tile_routed_moe_kernel(tc, xT, w1, w2, gate, offs, out):
@@ -70,18 +66,21 @@ def tile_routed_moe_kernel(tc, xT, w1, w2, gate, offs, out):
 
         slots_list = keep.tile([P, SLOTS // LIST_ROWS], U16, name="slots_list", align_bytes=64)
         pairs = [keep.tile([P, PAIR, SLOTS, PAIR], BF16, name=f"pairs{a}", align_bytes=64) for a in range(PASSES)]
-        x_grouped = [keep.tile([P, SLOTS * PACK], BF16, name=f"x_grouped{a}", align_bytes=64) for a in range(PASSES)]
         slot_words = [keep.tile([P, SLOTS], U32, name=f"slot_words{a}", align_bytes=64) for a in range(PASSES)]
         slot_scales = [keep.tile([P, SLOTS], U8, name=f"slot_scales{a}", align_bytes=64) for a in range(PASSES)]
         windows = [keep.tile([P, T], F32, name=f"window{b}", align_bytes=ALIGN) for b in range(OUT_TILES)]
 
         w1_raw, w2_raw, gate_sb = {}, {}, {}
 
-        def gather_rows(a, r):
-            rows = place([P, PAIR * T], F32, f"rows{a}_{r}", PASSES * BUFFER + ROWS * (PAIR * a + r))
-            nc.sync.dma_start(rows[:], xT.rearrange("(a p r s) n -> a r p (s n)", p=P, r=PAIR, s=PAIR)[a, r])
-            nc.scalar.activation(pairs[a][:, 0, :, r], rows[:].indirect(slots_list[:]), COPY)
-            nc.vector.tensor_copy(pairs[a][:, 1, :, r], rows[:, T:].indirect(slots_list[:]))
+        def offsets(first, end):
+            return slots_list[:, first // LIST_ROWS : end // LIST_ROWS]
+
+        def gather_plane(a, j):
+            plane = place([P, T], F32, f"plane{a}_{j}", PASSES * BUFFER + PLANE * (PACK * a + j))
+            nc.sync.dma_start(plane[:], xT.rearrange("(a p j) n -> a j p n", p=P, j=PACK)[a, j])
+            values = pairs[a][:, j // PAIR, :, j % PAIR]
+            nc.vector.tensor_copy(values[:, :X_VECTOR], plane[:].indirect(offsets(0, X_VECTOR)))
+            nc.scalar.activation(values[:, X_VECTOR:], plane[:].indirect(offsets(X_VECTOR, SLOTS)), COPY)
 
         def load_w1(e, a):
             w1_raw[e, a] = place([P, PACK, H], F32, f"w1_raw{e}_{a}", BUFFER * (PASSES * e + a))
@@ -99,8 +98,8 @@ def tile_routed_moe_kernel(tc, xT, w1, w2, gate, offs, out):
         nc.scalar.copy(windows[1][:], windows[0][:])
         nc.sync.dma_start(slots_list[:], offs)
         for a in range(PASSES):
-            for r in range(PAIR):
-                gather_rows(a, r)
+            for j in range(PACK):
+                gather_plane(a, j)
         for e in range(E):
             for a in range(PASSES):
                 load_w1(e, a)
@@ -114,26 +113,28 @@ def tile_routed_moe_kernel(tc, xT, w1, w2, gate, offs, out):
             for b in range(OUT_TILES):
                 load_gate(e, b)
 
-        def join_x(a, first, end, copy, word):
-            joined = x_grouped[a][:].bitcast(word).rearrange("p (c s) -> p c s", s=PAIR)
+        def join_x(a, g, copy, word, joined):
             halves = pairs[a][:].rearrange("p s c r -> p s (c r)").bitcast(word).rearrange("p s c -> p c s")
-            copy(joined[:, first:end], halves[:, first:end])
+            copy(
+                joined[:].bitcast(word).rearrange("p (c s) -> p c s", s=PAIR),
+                halves[:, GROUP * g : GROUP * (g + 1)],
+            )
+            return joined
 
-        def quantise_x(a, first, end):
+        def quantise_x(a, g, joined):
+            slots = slice(GROUP * g, GROUP * (g + 1))
             nc.vector.quantize_mx(
-                out=slot_words[a][:, first:end].bitcast(FP8X4),
-                scales=slot_scales[a][:, first:end],
-                in_=x_grouped[a][:, PACK * first : PACK * end],
+                out=slot_words[a][:, slots].bitcast(FP8X4), scales=slot_scales[a][:, slots], in_=joined[:]
             )
 
-        for a in range(PASSES):
-            for first in range(0, SLOTS, 2 * C):
-                if a == 0 and first > 0:
-                    join_x(a, first, first + 2 * C, nc.scalar.copy, U32)
-                else:
-                    join_x(a, first, first + 2 * C, nc.vector.tensor_copy, I32)
-            for first in range(0, SLOTS, 2 * C):
-                quantise_x(a, first, first + 2 * C)
+        def joined_tile(a, g):
+            return keep.tile([P, GROUP * PACK], BF16, name=f"joined{a}_{g}", align_bytes=64)
+
+        first = join_x(0, 0, nc.vector.tensor_copy, I32, joined_tile(0, 0))
+        second = join_x(0, 1, nc.vector.tensor_copy, I32, joined_tile(0, 1))
+        quantise_x(0, 0, first)
+        quantise_x(0, 1, second)
+        quantise_x(1, 0, join_x(1, 0, nc.vector.tensor_copy, I32, joined_tile(1, 0)))
 
         def round_w1(e, a):
             grouped = x_pool.tile([P, H, PACK], BF16, name="w1_grouped", align_bytes=64)
@@ -141,7 +142,7 @@ def tile_routed_moe_kernel(tc, xT, w1, w2, gate, offs, out):
             scalar = W1_SCALAR.get((e, a), 0)
             if scalar > 0:
                 interleave_w1(nc.scalar.copy, grouped[:], w1_raw[e, a][:], slice(0, scalar))
-            if e > 0 and a == 1:
+            if a == 1:
                 for pair in range(TILES // PAIR):
                     interleave_w1(nc.vector.tensor_copy, grouped[:], w1_raw[e, a][:], slice(scalar, groups), pair)
             elif scalar < groups:
@@ -153,7 +154,8 @@ def tile_routed_moe_kernel(tc, xT, w1, w2, gate, offs, out):
             step = P if e == LAST - 1 else N
             for first in range(0, N, step):
                 features = slice(first, first + step)
-                interleave(nc.vector.tensor_copy, grouped[:, features], w2_raw[e][:, :, features])
+                copy = nc.scalar.copy if e == 0 else nc.vector.tensor_copy
+                interleave(copy, grouped[:, features], w2_raw[e][:, :, features])
             return grouped
 
         def quantise(name, grouped, offset=None):
@@ -171,7 +173,7 @@ def tile_routed_moe_kernel(tc, xT, w1, w2, gate, offs, out):
         h_sums = {}
 
         def layer1(e, a, grouped):
-            step = H // PAIR if e > 0 and a == 1 else H
+            step = H // PAIR if a == 1 else H
             parts = [quantise(f"w1_{e}_{a}_{c}", grouped[:, c : c + step]) for c in range(0, H, step)]
             for u in range(BANKS):
                 if a == 0:
@@ -244,7 +246,7 @@ def tile_routed_moe_kernel(tc, xT, w1, w2, gate, offs, out):
         def scatter(e, b):
             first = C * e - (HANDED if (e, b) == (LAST, 0) else 0)
             end = C * (e + 1) - (HANDED if (e, b) == (LAST - 1, 0) else 0)
-            window = windows[b][:].indirect(slots_list[:, first // LIST_ROWS : end // LIST_ROWS])
+            window = windows[b][:].indirect(offsets(first, end))
             if (e, b) == (LAST, 0):
                 nc.vector.tensor_copy(window, gated[b][:, first:end])
             else:
@@ -252,8 +254,11 @@ def tile_routed_moe_kernel(tc, xT, w1, w2, gate, offs, out):
 
         for a in range(PASSES):
             layer1(0, a, round_w1(0, a))
-        layer1(1, 0, round_w1(1, 0))
-        h_grouped = activate(0, place([P, TILES * C], F32, "first_relu", BUFFER * PASSES)[:])
+        late = join_x(1, 1, nc.vector.tensor_copy, I32, place([P, GROUP * PACK], BF16, "late_joined", BUFFER))
+        grouped = round_w1(1, 0)
+        quantise_x(1, 1, late)
+        layer1(1, 0, grouped)
+        h_grouped = activate(0, h_pool.tile([P, TILES * C], F32, name="relu")[:])
         layer1(1, 1, round_w1(1, 1))
         layer2(0, h_grouped, round_w2(0))
         for e in range(1, LAST):

@@ -34,7 +34,8 @@ BUFFER = PACK * H * 4
 ALIGN = 256
 LAST = E - 1
 HANDED = 32
-W1_SCALAR = {(0, 0): 80, (0, 1): 56, (1, 1): 64}
+W1_SCALAR = {(0, 0): 80, (0, 1): 56}
+W2_VECTOR = 64
 
 
 def interleave(copy, grouped, raw):
@@ -134,7 +135,10 @@ def tile_routed_moe_kernel(tc, xT, w1, w2, gate, offs, out):
         second = join_x(0, 1, nc.vector.tensor_copy, I32, joined_tile(0, 1))
         quantise_x(0, 0, first)
         quantise_x(0, 1, second)
-        quantise_x(1, 0, join_x(1, 0, nc.vector.tensor_copy, I32, joined_tile(1, 0)))
+        first = join_x(1, 0, nc.vector.tensor_copy, I32, joined_tile(1, 0))
+        second = join_x(1, 1, nc.scalar.copy, U32, joined_tile(1, 1))
+        quantise_x(1, 0, first)
+        quantise_x(1, 1, second)
 
         def round_w1(e, a):
             grouped = x_pool.tile([P, H, PACK], BF16, name="w1_grouped", align_bytes=64)
@@ -151,11 +155,14 @@ def tile_routed_moe_kernel(tc, xT, w1, w2, gate, offs, out):
 
         def round_w2(e):
             grouped = h_pool.tile([P, N, PACK], BF16, name="w2_grouped", align_bytes=64)
+            if e == 0:
+                interleave(nc.vector.tensor_copy, grouped[:, :W2_VECTOR], w2_raw[e][:, :, :W2_VECTOR])
+                interleave(nc.scalar.copy, grouped[:, W2_VECTOR:], w2_raw[e][:, :, W2_VECTOR:])
+                return grouped
             step = P if e == LAST - 1 else N
             for first in range(0, N, step):
                 features = slice(first, first + step)
-                copy = nc.scalar.copy if e == 0 else nc.vector.tensor_copy
-                interleave(copy, grouped[:, features], w2_raw[e][:, :, features])
+                interleave(nc.vector.tensor_copy, grouped[:, features], w2_raw[e][:, :, features])
             return grouped
 
         def quantise(name, grouped, offset=None):
@@ -254,10 +261,7 @@ def tile_routed_moe_kernel(tc, xT, w1, w2, gate, offs, out):
 
         for a in range(PASSES):
             layer1(0, a, round_w1(0, a))
-        late = join_x(1, 1, nc.vector.tensor_copy, I32, place([P, GROUP * PACK], BF16, "late_joined", BUFFER))
-        grouped = round_w1(1, 0)
-        quantise_x(1, 1, late)
-        layer1(1, 0, grouped)
+        layer1(1, 0, round_w1(1, 0))
         h_grouped = activate(0, h_pool.tile([P, TILES * C], F32, name="relu")[:])
         layer1(1, 1, round_w1(1, 1))
         layer2(0, h_grouped, round_w2(0))

@@ -29,12 +29,12 @@ LIST_ROWS = 16
 SLOTS = E * C
 GROUP = 2 * C
 PLANE = T * 4
-X_VECTOR = 448
+X_VECTOR = (448, 448, 256, 512)
 BUFFER = PACK * H * 4
 ALIGN = 256
 LAST = E - 1
 HANDED = 32
-W1_SCALAR = {(0, 0): 80, (0, 1): 56}
+W1_SCALAR = {(0, 0): 88, (0, 1): 56}
 W2_VECTOR = 64
 
 
@@ -67,7 +67,7 @@ def tile_routed_moe_kernel(tc, xT, w1, w2, gate, offs, out):
 
         slots_list = keep.tile([P, SLOTS // LIST_ROWS], U16, name="slots_list", align_bytes=64)
         pairs = [keep.tile([P, PAIR, SLOTS, PAIR], BF16, name=f"pairs{a}", align_bytes=64) for a in range(PASSES)]
-        slot_words = [keep.tile([P, SLOTS], U32, name=f"slot_words{a}", align_bytes=64) for a in range(PASSES)]
+        slot_words = {}
         slot_scales = [keep.tile([P, SLOTS], U8, name=f"slot_scales{a}", align_bytes=64) for a in range(PASSES)]
         windows = [keep.tile([P, T], F32, name=f"window{b}", align_bytes=ALIGN) for b in range(OUT_TILES)]
 
@@ -80,8 +80,9 @@ def tile_routed_moe_kernel(tc, xT, w1, w2, gate, offs, out):
             plane = place([P, T], F32, f"plane{a}_{j}", PASSES * BUFFER + PLANE * (PACK * a + j))
             nc.sync.dma_start(plane[:], xT.rearrange("(a p j) n -> a j p n", p=P, j=PACK)[a, j])
             values = pairs[a][:, j // PAIR, :, j % PAIR]
-            nc.vector.tensor_copy(values[:, :X_VECTOR], plane[:].indirect(offsets(0, X_VECTOR)))
-            nc.scalar.activation(values[:, X_VECTOR:], plane[:].indirect(offsets(X_VECTOR, SLOTS)), COPY)
+            share = X_VECTOR[PAIR * a + j // PAIR]
+            nc.vector.tensor_copy(values[:, :share], plane[:].indirect(offsets(0, share)))
+            nc.scalar.activation(values[:, share:], plane[:].indirect(offsets(share, SLOTS)), COPY)
 
         def load_w1(e, a):
             w1_raw[e, a] = place([P, PACK, H], F32, f"w1_raw{e}_{a}", BUFFER * (PASSES * e + a))
@@ -104,11 +105,15 @@ def tile_routed_moe_kernel(tc, xT, w1, w2, gate, offs, out):
         for e in range(E):
             for a in range(PASSES):
                 load_w1(e, a)
-                if e >= 2 and a == 0:
-                    for b in range(OUT_TILES):
-                        load_gate(e - 2, b)
                 if e >= 1 and a == 1:
                     load_w2(e - 1)
+                if (e, a) == (1, 1):
+                    load_gate(0, 0)
+                if (e, a) == (2, 0):
+                    load_gate(0, 1)
+                if (e, a) == (LAST, 0):
+                    for b in range(OUT_TILES):
+                        load_gate(1, b)
         load_w2(LAST)
         for e in (LAST - 1, LAST):
             for b in range(OUT_TILES):
@@ -122,10 +127,15 @@ def tile_routed_moe_kernel(tc, xT, w1, w2, gate, offs, out):
             )
             return joined
 
-        def quantise_x(a, g, joined):
-            slots = slice(GROUP * g, GROUP * (g + 1))
+        def quantise_x(a, g, joined, offset=None):
+            if offset is None:
+                slot_words[a, g] = keep.tile([P, GROUP], U32, name=f"slot_words{a}_{g}", align_bytes=64)
+            else:
+                slot_words[a, g] = place([P, GROUP], U32, f"slot_words{a}_{g}", offset)
             nc.vector.quantize_mx(
-                out=slot_words[a][:, slots].bitcast(FP8X4), scales=slot_scales[a][:, slots], in_=joined[:]
+                out=slot_words[a, g][:].bitcast(FP8X4),
+                scales=slot_scales[a][:, GROUP * g : GROUP * (g + 1)],
+                in_=joined[:],
             )
 
         def joined_tile(a, g):
@@ -193,7 +203,7 @@ def tile_routed_moe_kernel(tc, xT, w1, w2, gate, offs, out):
                         out=h_sums[e, u][:, t],
                         lhsT=w1_words[:, columns].bitcast(FP8X4),
                         lhsT_scale=w1_scales[:, columns],
-                        rhs=slot_words[a][:, slots].bitcast(FP8X4),
+                        rhs=slot_words[a, slots.start // GROUP][:, slots.start % GROUP :][:, :BANK_SLOTS].bitcast(FP8X4),
                         rhs_scale=slot_scales[a][:, slots],
                         start=(a == 0 and t == 0),
                         stop=(a == PASSES - 1 and t == TILES - 1),

from contextlib import ExitStack

import concourse.mybir as mybir

K, T, E, C, H, N = 1024, 1536, 4, 256, 512, 256
FLOPS = 2 * E * C * (K * H + H * N)

F32 = mybir.dt.float32
BF16 = mybir.dt.bfloat16
I32 = mybir.dt.int32
U32 = mybir.dt.uint32
U16 = mybir.dt.uint16
U8 = mybir.dt.uint8
FP8X4 = mybir.dt.float8_e4m3fn_x4
MULT = mybir.AluOpType.mult
COPY = mybir.ActivationFunctionType.Copy
RELU = mybir.ActivationFunctionType.Relu
SQUARE = mybir.ActivationFunctionType.Square

P = 128
PACK = 4
PAIR = 2
PASSES = K // (P * PACK)
TILES = H // P
BANK_SLOTS = 128
BANKS = C // BANK_SLOTS
OUT_TILES = N // P
LIST_ROWS = 16
SLOTS = E * C
GROUP = 2 * C
PLANE = T * 4
X_VECTOR = (448, 448, 256, 512)
BUFFER = PACK * H * 4
ALIGN = 256
LAST = E - 1
HANDED = 32
W1_SCALAR = {(0, 0): 88, (0, 1): 56}
W2_VECTOR = 64


def interleave(copy, grouped, raw):
    copy(
        grouped.rearrange("p (c i) j -> p c j i", i=PACK),
        raw.rearrange("p j (c i) -> p c j i", i=PACK),
    )


def interleave_w1(copy, grouped, raw, groups, pair=slice(None)):
    copy(
        grouped.rearrange("p (u v m) j -> p u m j v", u=TILES // PAIR, v=PAIR)[:, pair, groups],
        raw.rearrange("p j (m u v) -> p u m j v", u=TILES // PAIR, v=PAIR)[:, pair, groups],
    )


def tile_routed_moe_kernel(tc, xT, w1, w2, gate, offs, out):
    nc = tc.nc
    with ExitStack() as ctx:
        keep = ctx.enter_context(tc.tile_pool(name="keep", bufs=1))
        placed = ctx.enter_context(tc.tile_pool(name="placed", bufs=1))
        x_pool = ctx.enter_context(tc.tile_pool(name="x_pool", bufs=3))
        h_pool = ctx.enter_context(tc.tile_pool(name="h_pool", bufs=2))
        h_psum = ctx.enter_context(tc.psum_pool(name="h_psum", bufs=2 * BANKS))
        y_psum = ctx.enter_context(tc.psum_pool(name="y_psum", bufs=2 * OUT_TILES))

        def place(shape, dtype, name, offset):
            return placed.tile(shape, dtype, name=name, align_bytes=ALIGN, offset=offset)

        slots_list = keep.tile([P, SLOTS // LIST_ROWS], U16, name="slots_list", align_bytes=64)
        pairs = [keep.tile([P, PAIR, SLOTS, PAIR], BF16, name=f"pairs{a}", align_bytes=64) for a in range(PASSES)]
        slot_words = {}
        slot_scales = [keep.tile([P, SLOTS], U8, name=f"slot_scales{a}", align_bytes=64) for a in range(PASSES)]
        windows = [keep.tile([P, T], F32, name=f"window{b}", align_bytes=ALIGN) for b in range(OUT_TILES)]

        w1_raw, w2_raw, gate_sb = {}, {}, {}

        def offsets(first, end):
            return slots_list[:, first // LIST_ROWS : end // LIST_ROWS]

        def gather_plane(a, j):
            plane = place([P, T], F32, f"plane{a}_{j}", PASSES * BUFFER + PLANE * (PACK * a + j))
            nc.sync.dma_start(plane[:], xT.rearrange("(a p j) n -> a j p n", p=P, j=PACK)[a, j])
            values = pairs[a][:, j // PAIR, :, j % PAIR]
            share = X_VECTOR[PAIR * a + j // PAIR]
            nc.vector.tensor_copy(values[:, :share], plane[:].indirect(offsets(0, share)))
            nc.scalar.activation(values[:, share:], plane[:].indirect(offsets(share, SLOTS)), COPY)

        def load_w1(e, a):
            w1_raw[e, a] = place([P, PACK, H], F32, f"w1_raw{e}_{a}", BUFFER * (PASSES * e + a))
            nc.sync.dma_start(w1_raw[e, a][:], w1[e].rearrange("(a p j) h -> a p j h", p=P, j=PACK)[a])

        def load_w2(e):
            w2_raw[e] = keep.tile([P, PACK, N], F32, name=f"w2_raw{e}", align_bytes=ALIGN)
            nc.sync.dma_start(w2_raw[e][:], w2[e].rearrange("(p t) n -> p t n", t=PACK))

        def load_gate(e, b):
            gate_sb[e, b] = keep.tile([P, C], F32, name=f"gate_sb{e}_{b}", align_bytes=ALIGN)
            nc.sync.dma_start(gate_sb[e, b][:], gate[P * b : P * (b + 1), C * e : C * (e + 1)])

        nc.vector.memset(windows[0][:], 0.0)
        nc.scalar.copy(windows[1][:], windows[0][:])
        nc.sync.dma_start(slots_list[:], offs)
        for a in range(PASSES):
            for j in range(PACK):
                gather_plane(a, j)
        for e in range(E):
            for a in range(PASSES):
                load_w1(e, a)
                if e >= 1 and a == 1:
                    load_w2(e - 1)
                if (e, a) == (1, 1):
                    load_gate(0, 0)
                if (e, a) == (2, 0):
                    load_gate(0, 1)
                if (e, a) == (LAST, 0):
                    for b in range(OUT_TILES):
                        load_gate(1, b)
        load_w2(LAST)
        for e in (LAST - 1, LAST):
            for b in range(OUT_TILES):
                load_gate(e, b)

        def join_x(a, g, copy, word, joined):
            halves = pairs[a][:].rearrange("p s c r -> p s (c r)").bitcast(word).rearrange("p s c -> p c s")
            copy(
                joined[:].bitcast(word).rearrange("p (c s) -> p c s", s=PAIR),
                halves[:, GROUP * g : GROUP * (g + 1)],
            )
            return joined

        def quantise_x(a, g, joined, offset=None):
            if offset is None:
                slot_words[a, g] = keep.tile([P, GROUP], U32, name=f"slot_words{a}_{g}", align_bytes=64)
            else:
                slot_words[a, g] = place([P, GROUP], U32, f"slot_words{a}_{g}", offset)
            nc.vector.quantize_mx(
                out=slot_words[a, g][:].bitcast(FP8X4),
                scales=slot_scales[a][:, GROUP * g : GROUP * (g + 1)],
                in_=joined[:],
            )

        def joined_tile(a, g):
            return keep.tile([P, GROUP * PACK], BF16, name=f"joined{a}_{g}", align_bytes=64)

        first = join_x(0, 0, nc.vector.tensor_copy, I32, joined_tile(0, 0))
        second = join_x(0, 1, nc.vector.tensor_copy, I32, joined_tile(0, 1))
        quantise_x(0, 0, first)
        quantise_x(0, 1, second)
        first = join_x(1, 0, nc.vector.tensor_copy, I32, joined_tile(1, 0))
        second = join_x(1, 1, nc.scalar.copy, U32, joined_tile(1, 1))
        quantise_x(1, 0, first)
        quantise_x(1, 1, second)

        def round_w1(e, a):
            grouped = x_pool.tile([P, H, PACK], BF16, name="w1_grouped", align_bytes=64)
            groups = P
            scalar = W1_SCALAR.get((e, a), 0)
            if scalar > 0:
                interleave_w1(nc.scalar.copy, grouped[:], w1_raw[e, a][:], slice(0, scalar))
            if a == 1:
                for pair in range(TILES // PAIR):
                    interleave_w1(nc.vector.tensor_copy, grouped[:], w1_raw[e, a][:], slice(scalar, groups), pair)
            elif scalar < groups:
                interleave_w1(nc.vector.tensor_copy, grouped[:], w1_raw[e, a][:], slice(scalar, groups))
            return grouped

        def round_w2(e):
            grouped = h_pool.tile([P, N, PACK], BF16, name="w2_grouped", align_bytes=64)
            if e == 0:
                interleave(nc.vector.tensor_copy, grouped[:, :W2_VECTOR], w2_raw[e][:, :, :W2_VECTOR])
                interleave(nc.scalar.copy, grouped[:, W2_VECTOR:], w2_raw[e][:, :, W2_VECTOR:])
                return grouped
            step = P if e == LAST - 1 else N
            for first in range(0, N, step):
                features = slice(first, first + step)
                interleave(nc.vector.tensor_copy, grouped[:, features], w2_raw[e][:, :, features])
            return grouped

        def quantise(name, grouped, offset=None):
            width = grouped.shape[1]
            if offset is None:
                codes = keep.tile([P, width], U32, name=f"{name}_words", align_bytes=64)
            else:
                codes = place([P, width], U32, f"{name}_words", offset)
            exponents = keep.tile([P, width], U8, name=f"{name}_scales", align_bytes=64)
            nc.vector.quantize_mx(
                out=codes[:].bitcast(FP8X4), scales=exponents[:], in_=grouped.rearrange("p c j -> p (c j)")
            )
            return codes, exponents

        h_sums = {}

        def layer1(e, a, grouped):
            step = H // PAIR if a == 1 else H
            parts = [quantise(f"w1_{e}_{a}_{c}", grouped[:, c : c + step]) for c in range(0, H, step)]
            for u in range(BANKS):
                if a == 0:
                    h_sums[e, u] = h_psum.tile([P, TILES, BANK_SLOTS], F32, name="h_sums")
                slots = slice(C * e + BANK_SLOTS * u, C * e + BANK_SLOTS * (u + 1))
                for t in range(TILES):
                    w1_words, w1_scales = parts[P * t // step]
                    columns = slice(P * t % step, P * t % step + P)
                    nc.tensor.matmul_mx(
                        out=h_sums[e, u][:, t],
                        lhsT=w1_words[:, columns].bitcast(FP8X4),
                        lhsT_scale=w1_scales[:, columns],
                        rhs=slot_words[a, slots.start // GROUP][:, slots.start % GROUP :][:, :BANK_SLOTS].bitcast(FP8X4),
                        rhs_scale=slot_scales[a][:, slots],
                        start=(a == 0 and t == 0),
                        stop=(a == PASSES - 1 and t == TILES - 1),
                    )

        def activate(e, flat):
            relu = flat.rearrange("p (m t s) -> p m t s", t=TILES, s=PAIR)
            grouped = h_pool.tile([P, C, PACK], BF16, name="h_grouped", align_bytes=64)
            banks = [(u, slice(0, BANK_SLOTS)) for u in range(BANKS)]
            if e == LAST:
                banks[-1:] = [(BANKS - 1, slice(n, n + BANK_SLOTS // 2)) for n in (0, BANK_SLOTS // 2)]
            places = [slice(BANK_SLOTS * u + part.start, BANK_SLOTS * u + part.stop) for u, part in banks]
            for (u, part), slots in zip(banks, places):
                sums = h_sums[e, u][:, :, part].rearrange("p t (m s) -> p m t s", s=PAIR)
                nc.scalar.activation(relu[:, slots.start // PAIR : slots.stop // PAIR], sums, RELU)
            for (u, part), slots in zip(banks, places):
                values = relu[:, slots.start // PAIR : slots.stop // PAIR].rearrange("p m t s -> p m s t")
                words = grouped[:, slots].rearrange("p (m s) t -> p m s t", s=PAIR)
                if (e, u) == (LAST, 0):
                    nc.vector.tensor_tensor(words, values, values, MULT)
                else:
                    nc.scalar.activation(words, values, SQUARE)
            return grouped

        y_sums = {}

        def layer2(e, h_grouped, w2_grouped):
            held = BUFFER * (PASSES * (e + 1) + (0 if e == LAST - 1 else 1))
            if e < LAST:
                parts = [(slice(0, C), quantise(f"h_{e}", h_grouped[:], held))]
            step = P if e == LAST - 1 else N
            w2_mx = [quantise(f"w2_{e}_{c}", w2_grouped[:, c : c + step]) for c in range(0, N, step)]
            if e == LAST:
                halves = [slice(BANK_SLOTS * u, BANK_SLOTS * (u + 1)) for u in range(BANKS)]
                parts = [(slots, quantise(f"h_{e}_{u}", h_grouped[:, slots])) for u, slots in enumerate(halves)]
            for b in range(OUT_TILES):
                y_sums[e, b] = y_psum.tile([P, C], F32, name="y_sums")
            for slots, (h_words, h_scales) in parts:
                for b in range(OUT_TILES):
                    w2_words, w2_scales = w2_mx[P * b // step]
                    features = slice(P * b % step, P * b % step + P)
                    nc.tensor.matmul_mx(
                        out=y_sums[e, b][:, slots],
                        lhsT=w2_words[:, features].bitcast(FP8X4),
                        lhsT_scale=w2_scales[:, features],
                        rhs=h_words[:].bitcast(FP8X4),
                        rhs_scale=h_scales[:],
                        start=True,
                        stop=True,
                    )

        gated = [keep.tile([P, E * C], F32, name=f"gated{b}", align_bytes=64) for b in range(OUT_TILES)]

        def apply_gate(e, b):
            nc.vector.tensor_tensor(gated[b][:, C * e : C * (e + 1)], y_sums[e, b][:], gate_sb[e, b][:], MULT)

        def scatter(e, b):
            first = C * e - (HANDED if (e, b) == (LAST, 0) else 0)
            end = C * (e + 1) - (HANDED if (e, b) == (LAST - 1, 0) else 0)
            window = windows[b][:].indirect(offsets(first, end))
            if (e, b) == (LAST, 0):
                nc.vector.tensor_copy(window, gated[b][:, first:end])
            else:
                nc.scalar.activation(window, gated[b][:, first:end], COPY)

        for a in range(PASSES):
            layer1(0, a, round_w1(0, a))
        layer1(1, 0, round_w1(1, 0))
        h_grouped = activate(0, h_pool.tile([P, TILES * C], F32, name="relu")[:])
        layer1(1, 1, round_w1(1, 1))
        layer2(0, h_grouped, round_w2(0))
        for e in range(1, LAST):
            h_grouped = activate(e, h_pool.tile([P, TILES * C], F32, name="relu")[:])
            grouped = round_w1(e + 1, 0)
            for b in range(OUT_TILES):
                apply_gate(e - 1, b)
                scatter(e - 1, b)
            layer1(e + 1, 0, grouped)
            layer1(e + 1, 1, round_w1(e + 1, 1))
            layer2(e, h_grouped, round_w2(e))
        apply_gate(LAST - 1, 0)
        h_grouped = activate(LAST, h_pool.tile([P, TILES * C], F32, name="relu")[:])
        scatter(LAST - 1, 0)
        w2_grouped = round_w2(LAST)
        layer2(LAST, h_grouped, w2_grouped)
        apply_gate(LAST - 1, 1)
        scatter(LAST - 1, 1)
        for b in range(OUT_TILES):
            apply_gate(LAST, b)
        for b in range(OUT_TILES):
            scatter(LAST, b)

        for b in range(OUT_TILES):
            nc.sync.dma_start(out[P * b : P * (b + 1), :], windows[b][:])
